import numpy as np
import ml_dtypes


def mxq(x, axis, fmt="e4m3"):
    dtype, down = {"e4m3": (ml_dtypes.float8_e4m3fn, 7), "e5m2": (ml_dtypes.float8_e5m2, 14)}[fmt]
    v = np.moveaxis(np.asarray(x, np.float32).astype(ml_dtypes.bfloat16).astype(np.float64), axis, -1)
    blocks = v.reshape(v.shape[:-1] + (-1, 32))
    amax = np.abs(blocks).max(-1, keepdims=True)
    byte = np.maximum(np.where(amax > 0, np.frexp(amax)[1] - 1 + 127, 0) - down, 1)
    scale = np.exp2(byte - 127.0)
    codes = (blocks / scale).astype(np.float32).astype(dtype).astype(np.float64)
    return np.moveaxis((codes * scale).reshape(v.shape), -1, axis)


WIDE = False


def mx_kscale(k):
    if not WIDE:
        return np.ones(k)
    levels = np.array([10, -10, 5, -5, 0])
    if k % 512:
        return np.exp2(np.random.permutation(np.resize(levels, k // 32))).repeat(32)
    a = np.empty((k // 512, 16))
    for p in range(k // 512):
        a[p, :8] = np.random.permutation(np.resize(levels, 8))
        for g in range(8):
            far = levels[np.abs(levels - a[p, g]) >= 10]
            a[p, g + 8] = far[np.random.randint(len(far))]
    return np.exp2(a.ravel()).repeat(32)


def f64(x):
    return np.asarray(x).astype(np.float64)


def striped(idx):
    return np.tile(idx.reshape(-1, 16).T, (8, 1)).astype(np.uint16)


def unstriped(offs):
    return offs[:16].T.reshape(-1).astype(np.int64)


def striped8(idx):
    return np.concatenate([x.reshape(-1, 16).T for x in idx]).astype(np.uint16)


def runs(offs, k):
    lists = np.stack([offs[16 * r : 16 * r + 16].T.reshape(-1) for r in range(8)]).astype(np.int64)
    return lists[np.arange(k) % 512 // 64]


def pack_weight(w):
    k, n = w.shape
    w = f64(np.asarray(w, np.float32).astype(ml_dtypes.bfloat16)).reshape(k // 32, 32, n)
    amax = np.abs(w).max(1)
    byte = np.clip(np.where(amax > 0, np.frexp(amax)[1] - 1 + 127 - 7, 1), 1, 254)
    scaled = (w * np.exp2(127.0 - byte)[:, None, :]).reshape(k, n).astype(np.float32)
    words = np.ascontiguousarray(scaled.reshape(k // 512, 128, 4, n).transpose(0, 1, 3, 2)).astype(ml_dtypes.float8_e4m3fn).view(np.uint8)
    return words, np.ascontiguousarray(byte.astype(np.uint8).reshape(k // 512, 16, n))


def unpack_weight(words, scales):
    g, p, n, _ = words.shape
    vals = np.ascontiguousarray(words).view(ml_dtypes.float8_e4m3fn).astype(np.float64) * np.repeat(np.exp2(scales.astype(np.float64) - 127.0), 8, axis=1)[..., None]
    return vals.transpose(0, 1, 3, 2).reshape(g * 512, n)


E2M1 = np.array([0.0, 0.5, 1.0, 1.5, 2.0, 3.0, 4.0, 6.0, -0.0, -0.5, -1.0, -1.5, -2.0, -3.0, -4.0, -6.0])


def pack_fp4(w):
    k, n = w.shape
    w = f64(np.asarray(w, np.float32).astype(ml_dtypes.bfloat16)).reshape(k // 32, 32, n)
    amax = np.abs(w).max(1)
    mant, ex = np.frexp(amax / 6.0)
    byte = np.clip(np.where(amax > 0, np.where(mant > 0.5, ex, ex - 1) + 127, 1), 1, 254)
    scaled = (w * np.exp2(127.0 - byte)[:, None, :]).reshape(k, n).astype(np.float32)
    c = np.ascontiguousarray(scaled.reshape(k // 512, 128, 4, n).transpose(0, 1, 3, 2)).astype(ml_dtypes.float4_e2m1fn).view(np.uint8) & 0xF
    words = (c[..., 0::2] | (c[..., 1::2] << 4)).reshape(k // 512, 128, 2 * n)
    return np.ascontiguousarray(words), np.ascontiguousarray(byte.astype(np.uint8).reshape(k // 512, 16, n))


def unpack_fp4(words, scales):
    g, _, n = scales.shape
    words = np.ascontiguousarray(words).reshape(g, 128, n, 2)
    nib = np.empty((g, 128, n, 4), np.uint8)
    nib[..., 0::2] = words & 0xF
    nib[..., 1::2] = words >> 4
    vals = E2M1[nib] * np.repeat(np.exp2(scales.astype(np.float64) - 127.0), 8, axis=1)[..., None]
    return vals.transpose(0, 1, 3, 2).reshape(g * 512, n)


K, T, S, H, N, V = 1024, 2048, 1024, 512, 128, 512


def setup_inputs():
    n = np.random.standard_normal
    s = mx_kscale(K)[:, None]
    u = mx_kscale(H)
    packed_xT = pack_weight(n((K, T)) * s)
    packed_w2 = pack_fp4(n((H, N)) / np.sqrt(H) / u[:, None])
    return {
        "x_words": packed_xT[0],
        "x_scales": packed_xT[1],
        "w1": (n((K, H)) / np.sqrt(K) / s * u).astype(np.float32),
        "w2_words": packed_w2[0],
        "w2_scales": packed_w2[1],
        "offs": striped8(np.stack([np.random.permutation(T)[:S] for _ in range(8)])),
        "left": striped(np.random.permutation(S)[:V]),
        "right": striped(np.random.permutation(S)[:V]),
    }


def reference(x_words, x_scales, w1, w2_words, w2_scales, offs, left, right):
    xq = unpack_weight(x_words, x_scales)[np.arange(K)[:, None], runs(offs, K)]
    h = mxq(f64(w1), 0, "e4m3").T @ xq
    z = np.abs(h[:, unstriped(left)] - h[:, unstriped(right)])
    return unpack_fp4(w2_words, w2_scales).T @ mxq(z, 0, "e4m3")

@@ -1,0 +1,215 @@
+from contextlib import ExitStack
+
+import concourse.mybir as mybir
+
+K, T, S, H, N, V = 1024, 2048, 1024, 512, 128, 512
+FLOPS = 2 * K * H * S + 2 * H * N * V
+
+F32 = mybir.dt.float32
+BF16 = mybir.dt.bfloat16
+I32 = mybir.dt.int32
+U32 = mybir.dt.uint32
+U16 = mybir.dt.uint16
+U8 = mybir.dt.uint8
+FP8X4 = mybir.dt.float8_e4m3fn_x4
+FP4X4 = mybir.dt.float4_e2m1fn_x4
+ABS = mybir.ActivationFunctionType.Abs
+SUB = mybir.AluOpType.subtract
+
+P = 128
+HALF = P // 2
+PASSES = K // 512
+STRIPE = 16
+
+
+def tile_picked_phpair_abs_p_kernel(
+    tc, x_words, x_scales, w1, w2_words, w2_scales, offs, left, right, out
+):
+    nc = tc.nc
+    with ExitStack() as ctx:
+        keep = ctx.enter_context(tc.tile_pool(name="keep", bufs=1))
+        psum = ctx.enter_context(tc.psum_pool(name="psum", bufs=1))
+
+        def sb(name, shape, dtype, tag=None):
+            return keep.tile(shape, dtype, name=name, tag=tag or name, align_bytes=64)
+
+        def bank(index, width):
+            return psum.tile([P, width], F32, name="bank%d" % index)
+
+        def entries(lists, start, stop):
+            return lists[:, start // STRIPE : stop // STRIPE]
+
+        offs_sb = keep.tile([P, S // STRIPE], U16, name="offs_sb")
+        left_sb = keep.tile([P, V // STRIPE], U16, name="left_sb")
+        right_sb = keep.tile([P, V // STRIPE], U16, name="right_sb")
+        xs_table = sb("xs_table", [P, T], U8)
+        xs_picked = sb("xs_picked", [P, S], U8)
+        xs_plane = sb("xs_plane", [P, PASSES, S], U8)
+        xw_table = [sb("xw_table%d" % g, [P, T], I32) for g in range(PASSES)]
+        xw_picked = [sb("xw_picked%d" % g, [P, S], U32) for g in range(PASSES)]
+        w1_raw = {(g, h): sb("w1_raw%d%d" % (g, h), [P, 4, 256], F32) for g in range(PASSES) for h in range(2)}
+        w2w = sb("w2w", [P, 2 * N], U8)
+
+        w1_view = w1.rearrange("(g p j) (h c) -> g h p j c", g=PASSES, j=4, h=2)
+
+        def load_words(g):
+            nc.sync.dma_start(xw_table[g][:], x_words[g].rearrange("p n t -> p (n t)").bitcast(I32))
+
+        def load_w1(g, h):
+            nc.sync.dma_start(w1_raw[g, h][:], w1_view[g, h])
+
+        nc.vector.memset(xs_table[:].bitcast(I32), 0)
+        nc.sync.dma_start(offs_sb[:], offs)
+        nc.sync.dma_start(left_sb[:], left)
+        nc.sync.dma_start(right_sb[:], right)
+        nc.sync.dma_start(w2w[:].bitcast(I32), w2_words[0].bitcast(I32))
+        nc.sync.dma_start(
+            xs_table[0:P:4, :].bitcast(I32), x_scales.rearrange("z q c -> q z c").bitcast(I32)
+        )
+        load_words(0)
+        load_w1(0, 0)
+        load_words(1)
+        load_w1(1, 0)
+        load_w1(0, 1)
+        load_w1(1, 1)
+
+        nc.vector.memset(xs_plane[:].rearrange("p g s -> p (g s)").bitcast(I32), 0)
+
+        nc.vector.tensor_copy(xs_picked[:], xs_table[:].indirect(offs_sb[:]))
+        for q in range(4):
+            nc.scalar.dma_start(
+                xs_plane[32 * q : 32 * q + 4, :, :].bitcast(I32),
+                xs_picked[32 * q : 32 * q + 32 : 4, :].bitcast(I32),
+            )
+
+        w2s = sb("w2s", [P, N], U8, tag="xs_picked")
+        nc.gpsimd.memset(w2s[:].bitcast(I32), 0)
+        for q in range(4):
+            nc.sync.dma_start(
+                w2s[32 * q : 32 * q + 4, :].bitcast(I32), w2_scales[0, 4 * q : 4 * q + 4, :].bitcast(I32)
+            )
+
+        def gather_words(g, start, stop):
+            nc.vector.tensor_copy(
+                xw_picked[g][:, start:stop],
+                xw_table[g][:].bitcast(U32).indirect(entries(offs_sb, start, stop)),
+            )
+
+        def round_w1(dst, g, h, t0):
+            src = w1_raw[g, h][:].rearrange("p j (m t) -> p m j t", t=4)[:, :, :, t0 : t0 + 2]
+            nc.scalar.copy(dst.rearrange("p t m j -> p m j t"), src)
+
+        def quantize(name, src, width):
+            codes = sb(name + "_codes", [P, width], U32)
+            scales = sb(name + "_scales", [P, width], U8)
+            nc.vector.quantize_mx(out=codes[:].bitcast(FP8X4), scales=scales[:], in_=src)
+            return codes, scales
+
+        wq = {}
+
+        def early_weights(name, g, h):
+            wb = sb("wb_%s%d" % (name, g), [P, 2, HALF, 4], BF16)
+            round_w1(wb[:], g, h, 0)
+            codes, scales = quantize("w%s%d" % (name, g), wb[:].rearrange("p t m j -> p (t m j)"), P)
+            wq[name, g] = (codes[:], scales[:])
+
+        def late_weights(g):
+            wb = sb("wb_late%d" % g, [P, 2, 2, HALF, 4], BF16)
+            for h in range(2):
+                round_w1(wb[:, :, h, :, :], g, h, 2)
+            codes, scales = quantize("wlate%d" % g, wb[:].rearrange("p t h m j -> p (t h m j)"), 2 * P)
+            wq["B", g] = (codes[:, 0:P], scales[:, 0:P])
+            wq["D", g] = (codes[:, P : 2 * P], scales[:, P : 2 * P])
+
+        def product_pass(acc, name, g, start, stop):
+            codes, scales = wq[name, g]
+            nc.tensor.matmul_mx(
+                out=acc[:],
+                lhsT=codes.bitcast(FP8X4),
+                lhsT_scale=scales,
+                rhs=xw_picked[g][:, start:stop].bitcast(FP8X4),
+                rhs_scale=xs_plane[:, g, start:stop],
+                start=(g == 0),
+                stop=(g == PASSES - 1),
+            )
+
+        h_sb = {name: sb("h" + name, [P, S], F32) for name in "ACBD"}
+
+        gather_words(0, 0, S)
+        early_weights("A", 0, 0)
+        pieces = [(0, 512), (512, 768), (768, 1024)]
+        acc_a = [bank(i, stop - start) for i, (start, stop) in enumerate(pieces)]
+        for acc, (start, stop) in zip(acc_a, pieces):
+            product_pass(acc, "A", 0, start, stop)
+        gather_words(1, *pieces[0])
+        gather_words(1, *pieces[1])
+        early_weights("A", 1, 0)
+        gather_words(1, *pieces[2])
+        for acc, (start, stop) in zip(acc_a, pieces):
+            product_pass(acc, "A", 1, start, stop)
+            nc.scalar.copy(h_sb["A"][:, start:stop], acc[:])
+
+        def project(name, first_bank):
+            for u in range(2):
+                acc = bank(first_bank + u, 512)
+                for g in range(PASSES):
+                    product_pass(acc, name, g, 512 * u, 512 * (u + 1))
+                nc.scalar.copy(h_sb[name][:, 512 * u : 512 * (u + 1)], acc[:])
+
+        for g in range(PASSES):
+            early_weights("C", g, 1)
+        project("C", 3)
+        for g in range(PASSES):
+            late_weights(g)
+        project("B", 5)
+        project("D", 0)
+
+        diff = sb("diff", [P, 4, V], F32)
+
+        def gather_left(name, start, stop):
+            picked = sb("left_%s%d" % (name, start), [P, stop - start], F32)
+            nc.vector.tensor_copy(picked[:], h_sb[name][:].indirect(entries(left_sb, start, stop)))
+            return picked
+
+        def subtract_right(dst, name, start, stop, picked):
+            nc.vector.tensor_tensor(dst, h_sb[name][:].indirect(entries(right_sb, start, stop)), picked[:], SUB)
+
+        for name, dst_rows in (("A", slice(0, HALF)), ("C", slice(HALF, P))):
+            d = sb("d" + name, [P, V], F32)
+            halves = [(0, V // 2), (V // 2, V)]
+            picked = [gather_left(name, a, b) for a, b in halves]
+            for (a, b), pk in zip(halves, picked):
+                subtract_right(d[:, a:b], name, a, b, pk)
+            for t in range(2):
+                nc.sync.dma_start(diff[dst_rows, t, :], d[HALF * t : HALF * (t + 1), :])
+
+        chunks = [(0, 256), (256, 384), (384, 512)]
+        out_banks = [7, 2, 3]
+        for c, (a, b) in enumerate(chunks):
+            n = b - a
+            picked = {name: gather_left(name, a, b) for name in "BD"}
+            for t, name in ((2, "B"), (3, "D")):
+                subtract_right(diff[:, t, a:b], name, a, b, picked[name])
+            zb = sb("zb%d" % c, [P, n, 4], BF16)
+            nc.scalar.activation(
+                zb[:].rearrange("p (c i) t -> p c t i", i=4),
+                diff[:, :, a:b].rearrange("p t (c i) -> p c t i", i=4),
+                ABS,
+            )
+            codes, scales = quantize("z%d" % c, zb[:].rearrange("p v t -> p (v t)"), n)
+            acc = bank(out_banks[c], n)
+            nc.tensor.matmul_mx(
+                out=acc[:],
+                lhsT=w2w[:].bitcast(FP4X4),
+                lhsT_scale=w2s[:],
+                rhs=codes[:].bitcast(FP8X4),
+                rhs_scale=scales[:],
+                start=True,
+                stop=True,
+            )
+            res = sb("res%d" % c, [P, n], F32)
+            if c == len(chunks) - 1:
+                nc.vector.tensor_copy(res[:], acc[:])
+            else:
+                nc.scalar.copy(res[:], acc[:])
+            nc.sync.dma_start(out[:, a:b], res[:])

@@ -47,7 +47,7 @@ def tile_picked_phpair_abs_p_kernel(
         xs_plane = sb("xs_plane", [P, PASSES, S], U8)
         xw_table = [sb("xw_table%d" % g, [P, T], I32) for g in range(PASSES)]
         xw_picked = [sb("xw_picked%d" % g, [P, S], U32) for g in range(PASSES)]
-        w1_raw = {(g, h): sb("w1_raw%d%d" % (g, h), [P, 4, 256], F32) for g in range(PASSES) for h in range(2)}
+        w1_raw = {}
         w2w = sb("w2w", [P, 2 * N], U8)
 
         w1_view = w1.rearrange("(g p j) (h c) -> g h p j c", g=PASSES, j=4, h=2)
@@ -55,7 +55,8 @@ def tile_picked_phpair_abs_p_kernel(
         def load_words(g):
             nc.sync.dma_start(xw_table[g][:], x_words[g].rearrange("p n t -> p (n t)").bitcast(I32))
 
-        def load_w1(g, h):
+        def load_w1(g, h, tag=None):
+            w1_raw[g, h] = sb("w1_raw%d%d" % (g, h), [P, 4, 256], F32, tag)
             nc.sync.dma_start(w1_raw[g, h][:], w1_view[g, h])
 
         nc.vector.memset(xs_table[:].bitcast(I32), 0)
@@ -69,25 +70,17 @@ def tile_picked_phpair_abs_p_kernel(
         load_words(0)
         load_w1(0, 0)
         load_words(1)
-        load_w1(1, 0)
-        load_w1(0, 1)
-        load_w1(1, 1)
 
         nc.vector.memset(xs_plane[:].rearrange("p g s -> p (g s)").bitcast(I32), 0)
 
         nc.vector.tensor_copy(xs_picked[:], xs_table[:].indirect(offs_sb[:]))
         for q in range(4):
-            nc.scalar.dma_start(
+            nc.sync.dma_start(
                 xs_plane[32 * q : 32 * q + 4, :, :].bitcast(I32),
                 xs_picked[32 * q : 32 * q + 32 : 4, :].bitcast(I32),
             )
 
-        w2s = sb("w2s", [P, N], U8, tag="xs_picked")
-        nc.gpsimd.memset(w2s[:].bitcast(I32), 0)
-        for q in range(4):
-            nc.sync.dma_start(
-                w2s[32 * q : 32 * q + 4, :].bitcast(I32), w2_scales[0, 4 * q : 4 * q + 4, :].bitcast(I32)
-            )
+        load_w1(1, 0, "xs_table")
 
         def gather_words(g, start, stop):
             nc.vector.tensor_copy(
@@ -136,6 +129,8 @@ def tile_picked_phpair_abs_p_kernel(
         h_sb = {name: sb("h" + name, [P, S], F32) for name in "ACBD"}
 
         gather_words(0, 0, S)
+        load_w1(0, 1, "xw_table0")
+        load_w1(1, 1, "xs_picked")
         early_weights("A", 0, 0)
         pieces = [(0, 512), (512, 768), (768, 1024)]
         acc_a = [bank(i, stop - start) for i, (start, stop) in enumerate(pieces)]
@@ -145,9 +140,16 @@ def tile_picked_phpair_abs_p_kernel(
         gather_words(1, *pieces[1])
         early_weights("A", 1, 0)
         gather_words(1, *pieces[2])
-        for acc, (start, stop) in zip(acc_a, pieces):
+        for acc, (start, stop), copy in zip(acc_a, pieces, (nc.vector.tensor_copy, nc.scalar.copy, nc.scalar.copy)):
             product_pass(acc, "A", 1, start, stop)
-            nc.scalar.copy(h_sb["A"][:, start:stop], acc[:])
+            copy(h_sb["A"][:, start:stop], acc[:])
+
+        w2s = sb("w2s", [P, N], U8, tag="xw_table1")
+        nc.gpsimd.memset(w2s[:].bitcast(I32), 0)
+        for q in range(4):
+            nc.sync.dma_start(
+                w2s[32 * q : 32 * q + 4, :].bitcast(I32), w2_scales[0, 4 * q : 4 * q + 4, :].bitcast(I32)
+            )
 
         def project(name, first_bank):
             for u in range(2):
@@ -164,40 +166,30 @@ def tile_picked_phpair_abs_p_kernel(
         project("B", 5)
         project("D", 0)
 
-        diff = sb("diff", [P, 4, V], F32)
+        CH = 128
+        diff = sb("diff", [P, V // CH, 4, CH], F32)
 
-        def gather_left(name, start, stop):
-            picked = sb("left_%s%d" % (name, start), [P, stop - start], F32)
+        def gather_left(name, start, stop, tag=None):
+            picked = sb("left_%s%d" % (name, start), [P, stop - start], F32, tag)
             nc.vector.tensor_copy(picked[:], h_sb[name][:].indirect(entries(left_sb, start, stop)))
             return picked
 
         def subtract_right(dst, name, start, stop, picked):
-            nc.vector.tensor_tensor(dst, h_sb[name][:].indirect(entries(right_sb, start, stop)), picked[:], SUB)
+            nc.vector.tensor_tensor(dst, h_sb[name][:].indirect(entries(right_sb, start, stop)), picked, SUB)
 
-        for name, dst_rows in (("A", slice(0, HALF)), ("C", slice(HALF, P))):
-            d = sb("d" + name, [P, V], F32)
-            halves = [(0, V // 2), (V // 2, V)]
-            picked = [gather_left(name, a, b) for a, b in halves]
-            for (a, b), pk in zip(halves, picked):
-                subtract_right(d[:, a:b], name, a, b, pk)
+        halves = [(0, V // 2), (V // 2, V)]
+        for name, dst_rows, left_tag, d_tag in (("A", slice(0, HALF), None, "wb_C1"), ("C", slice(HALF, P), "wb_late1", None)):
+            d = sb("d" + name, [P, V], F32, d_tag)
+            subtract_right(d[:], name, 0, V, gather_left(name, 0, V, left_tag)[:])
             for t in range(2):
-                nc.sync.dma_start(diff[dst_rows, t, :], d[HALF * t : HALF * (t + 1), :])
+                nc.sync.dma_start(
+                    diff[dst_rows, :, t, :], d[HALF * t : HALF * (t + 1), :].rearrange("p (c v) -> p c v", v=CH)
+                )
 
-        chunks = [(0, 256), (256, 384), (384, 512)]
-        out_banks = [7, 2, 3]
-        for c, (a, b) in enumerate(chunks):
+        def finish(index, zb, a, b, copy):
             n = b - a
-            picked = {name: gather_left(name, a, b) for name in "BD"}
-            for t, name in ((2, "B"), (3, "D")):
-                subtract_right(diff[:, t, a:b], name, a, b, picked[name])
-            zb = sb("zb%d" % c, [P, n, 4], BF16)
-            nc.scalar.activation(
-                zb[:].rearrange("p (c i) t -> p c t i", i=4),
-                diff[:, :, a:b].rearrange("p t (c i) -> p c t i", i=4),
-                ABS,
-            )
-            codes, scales = quantize("z%d" % c, zb[:].rearrange("p v t -> p (v t)"), n)
-            acc = bank(out_banks[c], n)
+            codes, scales = quantize("z%d" % index, zb.rearrange("p v t -> p (v t)"), n)
+            acc = bank((7, 2, 3)[index], n)
             nc.tensor.matmul_mx(
                 out=acc[:],
                 lhsT=w2w[:].bitcast(FP4X4),
@@ -207,9 +199,24 @@ def tile_picked_phpair_abs_p_kernel(
                 start=True,
                 stop=True,
             )
-            res = sb("res%d" % c, [P, n], F32)
-            if c == len(chunks) - 1:
-                nc.vector.tensor_copy(res[:], acc[:])
-            else:
-                nc.scalar.copy(res[:], acc[:])
+            res = sb("res%d" % index, [P, n], F32)
+            copy(res[:], acc[:])
             nc.sync.dma_start(out[:, a:b], res[:])
+
+        for u, (a, b) in enumerate(halves):
+            picked = {name: gather_left(name, a, b) for name in "BD"}
+            zb = sb("zb%d" % u, [P, b - a, 4], BF16)
+            for c in range(a // CH, b // CH):
+                lo = c * CH - a
+                for t, name in ((2, "B"), (3, "D")):
+                    subtract_right(diff[:, c, t, :], name, c * CH, (c + 1) * CH, picked[name][:, lo : lo + CH])
+                nc.scalar.activation(
+                    zb[:, lo : lo + CH, :].rearrange("p (c i) t -> p c t i", i=4),
+                    diff[:, c, :, :].rearrange("p t (c i) -> p c t i", i=4),
+                    ABS,
+                )
+                if u == 1:
+                    last = (c + 1) * CH == V
+                    finish(c - 1, zb[:, lo : lo + CH, :], c * CH, (c + 1) * CH, nc.vector.tensor_copy if last else nc.scalar.copy)
+            if u == 0:
+                finish(0, zb[:], a, b, nc.scalar.copy)

@@ -44,9 +44,9 @@ def tile_picked_phpair_abs_p_kernel(
         right_sb = keep.tile([P, V // STRIPE], U16, name="right_sb")
         xs_table = sb("xs_table", [P, T], U8)
         xs_picked = sb("xs_picked", [P, S], U8)
-        xs_plane = sb("xs_plane", [P, PASSES, S], U8)
+        xs_plane = sb("xs_plane", [P, S], U8)
         xw_table = [sb("xw_table%d" % g, [P, T], I32) for g in range(PASSES)]
-        xw_picked = [sb("xw_picked%d" % g, [P, S], U32) for g in range(PASSES)]
+        xw_picked = {}
         w1_raw = {}
         w2w = sb("w2w", [P, 2 * N], U8)
 
@@ -64,29 +64,31 @@ def tile_picked_phpair_abs_p_kernel(
         nc.sync.dma_start(left_sb[:], left)
         nc.sync.dma_start(right_sb[:], right)
         nc.sync.dma_start(w2w[:].bitcast(I32), w2_words[0].bitcast(I32))
-        nc.sync.dma_start(
-            xs_table[0:P:4, :].bitcast(I32), x_scales.rearrange("z q c -> q z c").bitcast(I32)
-        )
+        for e in range(2):
+            nc.sync.dma_start(
+                xs_table[e:P:8, :].bitcast(I32), x_scales.rearrange("z (r e) c -> e r z c", e=2)[e].bitcast(I32)
+            )
         load_words(0)
-        load_w1(0, 0)
         load_words(1)
+        load_w1(0, 0)
 
-        nc.vector.memset(xs_plane[:].rearrange("p g s -> p (g s)").bitcast(I32), 0)
 
         nc.vector.tensor_copy(xs_picked[:], xs_table[:].indirect(offs_sb[:]))
-        for q in range(4):
-            nc.sync.dma_start(
-                xs_plane[32 * q : 32 * q + 4, :, :].bitcast(I32),
-                xs_picked[32 * q : 32 * q + 32 : 4, :].bitcast(I32),
-            )
+        nc.vector.tensor_copy(xs_plane[:].bitcast(I32), xs_picked[:].bitcast(I32))
+        for e in range(2):
+            for g in range(PASSES):
+                nc.sync.dma_start(
+                    xs_plane[8 * g + 2 + e : P : 32, :].bitcast(I32),
+                    xs_picked[16 + 8 * g + e : P : 32, :].bitcast(I32),
+                )
 
         load_w1(1, 0, "xs_table")
 
-        def gather_words(g, start, stop):
-            nc.vector.tensor_copy(
-                xw_picked[g][:, start:stop],
-                xw_table[g][:].bitcast(U32).indirect(entries(offs_sb, start, stop)),
-            )
+        def gather_words(g, start, stop, tag=None):
+            picked = sb("xw_picked%d_%d" % (g, start), [P, stop - start], U32, tag)
+            nc.vector.tensor_copy(picked[:], xw_table[g][:].bitcast(U32).indirect(entries(offs_sb, start, stop)))
+            for u in range(start // 512, stop // 512):
+                xw_picked[g, u] = picked[:, 512 * u - start : 512 * (u + 1) - start]
 
         def round_w1(dst, g, h, t0):
             src = w1_raw[g, h][:].rearrange("p j (m t) -> p m j t", t=4)[:, :, :, t0 : t0 + 2]
@@ -120,8 +122,8 @@ def tile_picked_phpair_abs_p_kernel(
                 out=acc[:],
                 lhsT=codes.bitcast(FP8X4),
                 lhsT_scale=scales,
-                rhs=xw_picked[g][:, start:stop].bitcast(FP8X4),
-                rhs_scale=xs_plane[:, g, start:stop],
+                rhs=xw_picked[g, start // 512][:, start % 512 : (stop - 1) % 512 + 1].bitcast(FP8X4),
+                rhs_scale=xs_plane[8 * g : P, start:stop],
                 start=(g == 0),
                 stop=(g == PASSES - 1),
             )
@@ -131,15 +133,14 @@ def tile_picked_phpair_abs_p_kernel(
         gather_words(0, 0, S)
         load_w1(0, 1, "xw_table0")
         load_w1(1, 1, "xs_picked")
+        gather_words(1, 0, S // 2)
         early_weights("A", 0, 0)
+        gather_words(1, S // 2, S, "wb_A0")
         pieces = [(0, 512), (512, 768), (768, 1024)]
         acc_a = [bank(i, stop - start) for i, (start, stop) in enumerate(pieces)]
         for acc, (start, stop) in zip(acc_a, pieces):
             product_pass(acc, "A", 0, start, stop)
-        gather_words(1, *pieces[0])
-        gather_words(1, *pieces[1])
         early_weights("A", 1, 0)
-        gather_words(1, *pieces[2])
         for acc, (start, stop), copy in zip(acc_a, pieces, (nc.vector.tensor_copy, nc.scalar.copy, nc.scalar.copy)):
             product_pass(acc, "A", 1, start, stop)
             copy(h_sb["A"][:, start:stop], acc[:])

@@ -44,11 +44,10 @@ def tile_picked_phpair_abs_p_kernel(
         right_sb = keep.tile([P, V // STRIPE], U16, name="right_sb")
         xs_table = sb("xs_table", [P, T], U8)
         xs_picked = sb("xs_picked", [P, S], U8)
-        xs_plane = sb("xs_plane", [P, S], U8)
+        xs_plane = sb("xs_plane", [P, PASSES, S], U8)
         xw_table = [sb("xw_table%d" % g, [P, T], I32) for g in range(PASSES)]
-        xw_picked = {}
+        xw_picked = [[] for g in range(PASSES)]
         w1_raw = {}
-        w2w = sb("w2w", [P, 2 * N], U8)
 
         w1_view = w1.rearrange("(g p j) (h c) -> g h p j c", g=PASSES, j=4, h=2)
 
@@ -56,42 +55,41 @@ def tile_picked_phpair_abs_p_kernel(
             nc.sync.dma_start(xw_table[g][:], x_words[g].rearrange("p n t -> p (n t)").bitcast(I32))
 
         def load_w1(g, h, tag=None):
-            w1_raw[g, h] = sb("w1_raw%d%d" % (g, h), [P, 4, 256], F32, tag)
-            nc.sync.dma_start(w1_raw[g, h][:], w1_view[g, h])
+            raw = sb("w1_raw%d%d" % (g, h), [P, 4, 256], F32, tag)
+            w1_raw[g, h] = raw[:]
+            nc.sync.dma_start(raw[:], w1_view[g, h])
 
+        w2w = sb("w2w", [P, 2 * N], U8)
+        warm = sb("warm", [P, 2], F32)
+        nc.gpsimd.memset(warm[:, 0:1], 0.0)
+        nc.scalar.activation(warm[:, 1:2], warm[:, 0:1], ABS)
         nc.vector.memset(xs_table[:].bitcast(I32), 0)
+        nc.vector.memset(xs_plane[:].rearrange("p g s -> p (g s)").bitcast(I32), 0)
         nc.sync.dma_start(offs_sb[:], offs)
         nc.sync.dma_start(left_sb[:], left)
         nc.sync.dma_start(right_sb[:], right)
         nc.sync.dma_start(w2w[:].bitcast(I32), w2_words[0].bitcast(I32))
-        for e in range(2):
-            nc.sync.dma_start(
-                xs_table[e:P:8, :].bitcast(I32), x_scales.rearrange("z (r e) c -> e r z c", e=2)[e].bitcast(I32)
-            )
+        nc.sync.dma_start(xs_table[0:P:4, :].bitcast(I32), x_scales.rearrange("z r c -> r z c").bitcast(I32))
         load_words(0)
         load_words(1)
         load_w1(0, 0)
 
-
         nc.vector.tensor_copy(xs_picked[:], xs_table[:].indirect(offs_sb[:]))
-        nc.vector.tensor_copy(xs_plane[:].bitcast(I32), xs_picked[:].bitcast(I32))
-        for e in range(2):
-            for g in range(PASSES):
-                nc.sync.dma_start(
-                    xs_plane[8 * g + 2 + e : P : 32, :].bitcast(I32),
-                    xs_picked[16 + 8 * g + e : P : 32, :].bitcast(I32),
-                )
+        for q in range(4):
+            nc.scalar.dma_start(
+                xs_plane[32 * q : 32 * q + 4, :, :].rearrange("p g s -> p (g s)").bitcast(I32),
+                xs_picked[32 * q : 32 * q + 32 : 4, :].bitcast(I32),
+            )
 
         load_w1(1, 0, "xs_table")
 
         def gather_words(g, start, stop, tag=None):
             picked = sb("xw_picked%d_%d" % (g, start), [P, stop - start], U32, tag)
             nc.vector.tensor_copy(picked[:], xw_table[g][:].bitcast(U32).indirect(entries(offs_sb, start, stop)))
-            for u in range(start // 512, stop // 512):
-                xw_picked[g, u] = picked[:, 512 * u - start : 512 * (u + 1) - start]
+            xw_picked[g].append((start, stop, picked))
 
         def round_w1(dst, g, h, t0):
-            src = w1_raw[g, h][:].rearrange("p j (m t) -> p m j t", t=4)[:, :, :, t0 : t0 + 2]
+            src = w1_raw[g, h].rearrange("p j (m t) -> p m j t", t=4)[:, :, :, t0 : t0 + 2]
             nc.scalar.copy(dst.rearrange("p t m j -> p m j t"), src)
 
         def quantize(name, src, width):
@@ -108,22 +106,30 @@ def tile_picked_phpair_abs_p_kernel(
             codes, scales = quantize("w%s%d" % (name, g), wb[:].rearrange("p t m j -> p (t m j)"), P)
             wq[name, g] = (codes[:], scales[:])
 
-        def late_weights(g):
-            wb = sb("wb_late%d" % g, [P, 2, 2, HALF, 4], BF16)
-            for h in range(2):
-                round_w1(wb[:, :, h, :, :], g, h, 2)
-            codes, scales = quantize("wlate%d" % g, wb[:].rearrange("p t h m j -> p (t h m j)"), 2 * P)
-            wq["B", g] = (codes[:, 0:P], scales[:, 0:P])
-            wq["D", g] = (codes[:, P : 2 * P], scales[:, P : 2 * P])
+        wb_late = sb("wb_late", [P, PASSES, 2 * 2 * HALF * 4], BF16)
+
+        def late_weights():
+            parts = wb_late[:].rearrange("p g (t h m j) -> p g t h m j", t=2, h=2, j=4)
+            for g in range(PASSES):
+                round_w1(parts[:, g, :, 0, :, :], g, 0, 2)
+            nc.scalar.copy(
+                parts[:, :, :, 1, :, :].rearrange("p g t m j -> p g m j t"),
+                w1_second[:].rearrange("p g j (m t) -> p g m j t", t=4)[:, :, :, :, 2:4],
+            )
+            for g in range(PASSES):
+                codes, scales = quantize("wlate%d" % g, wb_late[:, g, :], 2 * P)
+                wq["B", g] = (codes[:, 0:P], scales[:, 0:P])
+                wq["D", g] = (codes[:, P : 2 * P], scales[:, P : 2 * P])
 
         def product_pass(acc, name, g, start, stop):
             codes, scales = wq[name, g]
+            first, picked = [(lo, tile) for lo, hi, tile in xw_picked[g] if lo <= start and stop <= hi][0]
             nc.tensor.matmul_mx(
-                out=acc[:],
+                out=acc,
                 lhsT=codes.bitcast(FP8X4),
                 lhsT_scale=scales,
-                rhs=xw_picked[g, start // 512][:, start % 512 : (stop - 1) % 512 + 1].bitcast(FP8X4),
-                rhs_scale=xs_plane[8 * g : P, start:stop],
+                rhs=picked[:, start - first : stop - first].bitcast(FP8X4),
+                rhs_scale=xs_plane[:, g, start:stop],
                 start=(g == 0),
                 stop=(g == PASSES - 1),
             )
@@ -131,44 +137,47 @@ def tile_picked_phpair_abs_p_kernel(
         h_sb = {name: sb("h" + name, [P, S], F32) for name in "ACBD"}
 
         gather_words(0, 0, S)
-        load_w1(0, 1, "xw_table0")
-        load_w1(1, 1, "xs_picked")
-        gather_words(1, 0, S // 2)
+        w1_second = sb("w1_second", [P, PASSES, 4, 256], F32, "xw_table0")
+        for g in range(PASSES):
+            w1_raw[g, 1] = w1_second[:, g, :, :]
+            nc.sync.dma_start(w1_raw[g, 1], w1_view[g, 1])
+        CUT = 768
+        gather_words(1, 0, CUT)
         early_weights("A", 0, 0)
-        gather_words(1, S // 2, S, "wb_A0")
-        pieces = [(0, 512), (512, 768), (768, 1024)]
-        acc_a = [bank(i, stop - start) for i, (start, stop) in enumerate(pieces)]
+        gather_words(1, CUT, S, "wb_A0")
+        pieces = [(start, start + 256) for start in range(0, S, 256)]
+        acc_a = [bank(i, 256) for i in range(4)]
         for acc, (start, stop) in zip(acc_a, pieces):
-            product_pass(acc, "A", 0, start, stop)
+            product_pass(acc[:], "A", 0, start, stop)
         early_weights("A", 1, 0)
-        for acc, (start, stop), copy in zip(acc_a, pieces, (nc.vector.tensor_copy, nc.scalar.copy, nc.scalar.copy)):
-            product_pass(acc, "A", 1, start, stop)
+        for acc, (start, stop), copy in zip(acc_a, pieces, (nc.vector.tensor_copy, nc.scalar.copy, nc.vector.tensor_copy, nc.vector.tensor_copy)):
+            product_pass(acc[:], "A", 1, start, stop)
             copy(h_sb["A"][:, start:stop], acc[:])
 
         w2s = sb("w2s", [P, N], U8, tag="xw_table1")
-        nc.gpsimd.memset(w2s[:].bitcast(I32), 0)
+        nc.vector.memset(w2s[:].bitcast(I32), 0)
         for q in range(4):
             nc.sync.dma_start(
                 w2s[32 * q : 32 * q + 4, :].bitcast(I32), w2_scales[0, 4 * q : 4 * q + 4, :].bitcast(I32)
             )
 
-        def project(name, first_bank):
-            for u in range(2):
-                acc = bank(first_bank + u, 512)
+        def project(index, name, start, stop):
+            acc = bank(index, stop - start)
+            cuts = [start] + [c for c in (CUT,) if start < c < stop] + [stop]
+            for lo, hi in zip(cuts, cuts[1:]):
                 for g in range(PASSES):
-                    product_pass(acc, name, g, 512 * u, 512 * (u + 1))
-                nc.scalar.copy(h_sb[name][:, 512 * u : 512 * (u + 1)], acc[:])
+                    product_pass(acc[:, lo - start : hi - start], name, g, lo, hi)
+            nc.scalar.copy(h_sb[name][:, start:stop], acc[:])
 
         for g in range(PASSES):
             early_weights("C", g, 1)
-        project("C", 3)
-        for g in range(PASSES):
-            late_weights(g)
-        project("B", 5)
-        project("D", 0)
+        project(4, "C", 0, 512)
+        project(5, "C", 512, S)
+        late_weights()
+        for index, name, start, stop in ((6, "B", 0, 512), (7, "D", 0, 512), (0, "D", 512, 768), (1, "B", 512, S), (2, "D", 768, S)):
+            project(index, name, start, stop)
 
         CH = 128
-        diff = sb("diff", [P, V // CH, 4, CH], F32)
 
         def gather_left(name, start, stop, tag=None):
             picked = sb("left_%s%d" % (name, start), [P, stop - start], F32, tag)
@@ -178,19 +187,49 @@ def tile_picked_phpair_abs_p_kernel(
         def subtract_right(dst, name, start, stop, picked):
             nc.vector.tensor_tensor(dst, h_sb[name][:].indirect(entries(right_sb, start, stop)), picked, SUB)
 
-        halves = [(0, V // 2), (V // 2, V)]
-        for name, dst_rows, left_tag, d_tag in (("A", slice(0, HALF), None, "wb_C1"), ("C", slice(HALF, P), "wb_late1", None)):
-            d = sb("d" + name, [P, V], F32, d_tag)
-            subtract_right(d[:], name, 0, V, gather_left(name, 0, V, left_tag)[:])
-            for t in range(2):
-                nc.sync.dma_start(
-                    diff[dst_rows, :, t, :], d[HALF * t : HALF * (t + 1), :].rearrange("p (c v) -> p c v", v=CH)
-                )
+        late = sb("diff_late", [P, 2, 4, CH], F32)
+        early = sb("diff_early", [P, 4, 2 * CH], F32)
+        diff = {0: early[:], 256: late[:, 0, :, :], 384: late[:, 1, :, :]}
 
-        def finish(index, zb, a, b, copy):
-            n = b - a
-            codes, scales = quantize("z%d" % index, zb.rearrange("p v t -> p (v t)"), n)
-            acc = bank((7, 2, 3)[index], n)
+        def move_rows(dst_rows, d, start):
+            for t in range(2):
+                src = d[HALF * t : HALF * (t + 1), start : start + 2 * CH]
+                if start == 0:
+                    nc.sync.dma_start(early[dst_rows, t, :], src)
+                else:
+                    nc.sync.dma_start(late[dst_rows, :, t, :], src.rearrange("p (c v) -> p c v", v=CH))
+
+        d_a = wb_late[:, 0, :].bitcast(F32)
+        subtract_right(d_a, "A", 0, V, gather_left("A", 0, V, "wb_C1")[:])
+        for start in (0, V // 2):
+            move_rows(slice(0, HALF), d_a, start)
+        d_c = sb("d_c", [P, V], F32)
+        halves = [(0, V // 2), (V // 2, V)]
+        left_c = [gather_left("C", start, stop) for start, stop in halves]
+        for picked, (start, stop) in zip(left_c, halves):
+            subtract_right(d_c[:, start:stop], "C", start, stop, picked[:])
+            move_rows(slice(HALF, P), d_c[:], start)
+
+        zb = [sb("zb%d" % i, [P, width, 4], BF16) for i, width in enumerate((256, 128, 128))]
+
+        def take_abs(index, start):
+            nc.scalar.activation(
+                zb[index][:].rearrange("p (c i) t -> p c t i", i=4),
+                diff[start].rearrange("p t (c i) -> p c t i", i=4),
+                ABS,
+            )
+
+        def finish(index, a, cuts, copy):
+            n = cuts[-1]
+            codes = sb("z_codes%d" % index, [P, n], U32)
+            scales = sb("z_scales%d" % index, [P, n], U8)
+            for lo, hi in zip([0] + cuts, cuts):
+                nc.vector.quantize_mx(
+                    out=codes[:, lo:hi].bitcast(FP8X4),
+                    scales=scales[:, lo:hi],
+                    in_=zb[index][:, lo:hi, :].rearrange("p v t -> p (v t)"),
+                )
+            acc = bank(3 + index, n)
             nc.tensor.matmul_mx(
                 out=acc[:],
                 lhsT=w2w[:].bitcast(FP4X4),
@@ -202,22 +241,22 @@ def tile_picked_phpair_abs_p_kernel(
             )
             res = sb("res%d" % index, [P, n], F32)
             copy(res[:], acc[:])
-            nc.sync.dma_start(out[:, a:b], res[:])
+            nc.sync.dma_start(out[:, a : a + n], res[:])
 
-        for u, (a, b) in enumerate(halves):
-            picked = {name: gather_left(name, a, b) for name in "BD"}
-            zb = sb("zb%d" % u, [P, b - a, 4], BF16)
-            for c in range(a // CH, b // CH):
-                lo = c * CH - a
-                for t, name in ((2, "B"), (3, "D")):
-                    subtract_right(diff[:, c, t, :], name, c * CH, (c + 1) * CH, picked[name][:, lo : lo + CH])
-                nc.scalar.activation(
-                    zb[:, lo : lo + CH, :].rearrange("p (c i) t -> p c t i", i=4),
-                    diff[:, c, :, :].rearrange("p t (c i) -> p c t i", i=4),
-                    ABS,
-                )
-                if u == 1:
-                    last = (c + 1) * CH == V
-                    finish(c - 1, zb[:, lo : lo + CH, :], c * CH, (c + 1) * CH, nc.vector.tensor_copy if last else nc.scalar.copy)
-            if u == 0:
-                finish(0, zb[:], a, b, nc.scalar.copy)
+        plane = {"B": 2, "D": 3}
+        lefts = ctx.enter_context(tc.tile_pool(name="lefts", bufs=2))
+        for names, a, cuts in (("BD", 0, (256,)), ("DB", 256, (384, 512))):
+            picked = {}
+            for name in names:
+                picked[name] = lefts.tile([P, cuts[-1] - a], F32, name="left_%s%d" % (name, a), tag="left")
+                nc.vector.tensor_copy(picked[name][:], h_sb[name][:].indirect(entries(left_sb, a, cuts[-1])))
+            for lo, hi in zip((a,) + cuts, cuts):
+                for name in names:
+                    subtract_right(
+                        diff[lo][:, plane[name], :],
+                        name, lo, hi, picked[name][:, lo - a : hi - a],
+                    )
+                take_abs((0, 256, 384).index(lo), lo)
+        finish(0, 0, [256], nc.scalar.copy)
+        finish(1, 256, [128], nc.vector.tensor_copy)
+        finish(2, 384, [128], nc.vector.tensor_copy)

@@ -60,10 +60,8 @@ def tile_picked_phpair_abs_p_kernel(
             nc.sync.dma_start(raw[:], w1_view[g, h])
 
         w2w = sb("w2w", [P, 2 * N], U8)
-        warm = sb("warm", [P, 2], F32)
-        nc.gpsimd.memset(warm[:, 0:1], 0.0)
-        nc.scalar.activation(warm[:, 1:2], warm[:, 0:1], ABS)
-        nc.vector.memset(xs_table[:].bitcast(I32), 0)
+        nc.vector.memset(xs_table[:, 0 : T // 2].bitcast(I32), 0)
+        nc.gpsimd.memset(xs_table[:, T // 2 : T].bitcast(I32), 0)
         nc.vector.memset(xs_plane[:].rearrange("p g s -> p (g s)").bitcast(I32), 0)
         nc.sync.dma_start(offs_sb[:], offs)
         nc.sync.dma_start(left_sb[:], left)
@@ -76,7 +74,7 @@ def tile_picked_phpair_abs_p_kernel(
 
         nc.vector.tensor_copy(xs_picked[:], xs_table[:].indirect(offs_sb[:]))
         for q in range(4):
-            nc.scalar.dma_start(
+            nc.sync.dma_start(
                 xs_plane[32 * q : 32 * q + 4, :, :].rearrange("p g s -> p (g s)").bitcast(I32),
                 xs_picked[32 * q : 32 * q + 32 : 4, :].bitcast(I32),
             )
@@ -258,5 +256,5 @@ def tile_picked_phpair_abs_p_kernel(
                     )
                 take_abs((0, 256, 384).index(lo), lo)
         finish(0, 0, [256], nc.scalar.copy)
-        finish(1, 256, [128], nc.vector.tensor_copy)
+        finish(1, 256, [128], nc.scalar.copy)
         finish(2, 384, [128], nc.vector.tensor_copy)

@@ -18,8 +18,13 @@ SUB = mybir.AluOpType.subtract
 
 P = 128
 HALF = P // 2
-PASSES = K // 512
+PACK = 4
+PASSES = K // (P * PACK)
 STRIPE = 16
+BANK = 512
+ZEROED_BY_VECTOR = 1216
+PAIR_HALVES = ((0, V // 2), (V // 2, V))
+CHUNKS = ((0, 256), (256, 384), (384, 512))
 
 
 def tile_picked_phpair_abs_p_kernel(
@@ -30,231 +35,227 @@ def tile_picked_phpair_abs_p_kernel(
         keep = ctx.enter_context(tc.tile_pool(name="keep", bufs=1))
         psum = ctx.enter_context(tc.psum_pool(name="psum", bufs=1))
 
-        def sb(name, shape, dtype, tag=None):
+        def sbuf_tile(name, shape, dtype, tag=None):
             return keep.tile(shape, dtype, name=name, tag=tag or name, align_bytes=64)
 
-        def bank(index, width):
+        def psum_bank(index, width):
             return psum.tile([P, width], F32, name="bank%d" % index)
 
-        def entries(lists, start, stop):
-            return lists[:, start // STRIPE : stop // STRIPE]
+        def entries(list_tile, start, stop):
+            return list_tile[:, start // STRIPE : stop // STRIPE]
 
         offs_sb = keep.tile([P, S // STRIPE], U16, name="offs_sb")
         left_sb = keep.tile([P, V // STRIPE], U16, name="left_sb")
         right_sb = keep.tile([P, V // STRIPE], U16, name="right_sb")
-        xs_table = sb("xs_table", [P, T], U8)
-        xs_picked = sb("xs_picked", [P, S], U8)
-        xs_plane = sb("xs_plane", [P, PASSES, S], U8)
-        xw_table = [sb("xw_table%d" % g, [P, T], I32) for g in range(PASSES)]
-        xw_picked = [[] for g in range(PASSES)]
+        scale_table = sbuf_tile("scale_table", [P, T], U8)
+        scales_picked = sbuf_tile("scales_picked", [P, S], U8)
+        x_scales_mx = sbuf_tile("x_scales_mx", [P, PASSES, S], U8)
+        word_table = [sbuf_tile("word_table%d" % g, [P, T], I32) for g in range(PASSES)]
+
+        w1_parts = w1.rearrange("(g p j) (h c) -> g h p j c", g=PASSES, j=PACK, h=2)
         w1_raw = {}
 
-        w1_view = w1.rearrange("(g p j) (h c) -> g h p j c", g=PASSES, j=4, h=2)
-
         def load_words(g):
-            nc.sync.dma_start(xw_table[g][:], x_words[g].rearrange("p n t -> p (n t)").bitcast(I32))
+            nc.sync.dma_start(word_table[g][:], x_words[g].rearrange("p n t -> p (n t)").bitcast(I32))
 
-        def load_w1(g, h, tag=None):
-            raw = sb("w1_raw%d%d" % (g, h), [P, 4, 256], F32, tag)
-            w1_raw[g, h] = raw[:]
-            nc.sync.dma_start(raw[:], w1_view[g, h])
+        def load_first_half(g, tag=None):
+            raw = sbuf_tile("w1_first%d" % g, [P, PACK, H // 2], F32, tag)
+            w1_raw[g, 0] = raw[:]
+            nc.sync.dma_start(raw[:], w1_parts[g, 0])
 
-        w2w = sb("w2w", [P, 2 * N], U8)
-        nc.vector.memset(xs_table[:, 0 : T // 2].bitcast(I32), 0)
-        nc.gpsimd.memset(xs_table[:, T // 2 : T].bitcast(I32), 0)
-        nc.vector.memset(xs_plane[:].rearrange("p g s -> p (g s)").bitcast(I32), 0)
+        nc.vector.memset(scale_table[:, 0:ZEROED_BY_VECTOR].bitcast(I32), 0)
+        nc.gpsimd.memset(scale_table[:, ZEROED_BY_VECTOR:T].bitcast(I32), 0)
+        nc.vector.memset(x_scales_mx[:].rearrange("p g s -> p (g s)").bitcast(I32), 0)
+
         nc.sync.dma_start(offs_sb[:], offs)
         nc.sync.dma_start(left_sb[:], left)
         nc.sync.dma_start(right_sb[:], right)
-        nc.sync.dma_start(w2w[:].bitcast(I32), w2_words[0].bitcast(I32))
-        nc.sync.dma_start(xs_table[0:P:4, :].bitcast(I32), x_scales.rearrange("z r c -> r z c").bitcast(I32))
+        nc.sync.dma_start(scale_table[0:P:4, :].bitcast(I32), x_scales.rearrange("z r c -> r z c").bitcast(I32))
         load_words(0)
+        load_first_half(0)
         load_words(1)
-        load_w1(0, 0)
 
-        nc.vector.tensor_copy(xs_picked[:], xs_table[:].indirect(offs_sb[:]))
+        nc.vector.tensor_copy(scales_picked[:], scale_table[:].indirect(offs_sb[:]))
         for q in range(4):
             nc.sync.dma_start(
-                xs_plane[32 * q : 32 * q + 4, :, :].rearrange("p g s -> p (g s)").bitcast(I32),
-                xs_picked[32 * q : 32 * q + 32 : 4, :].bitcast(I32),
+                x_scales_mx[32 * q : 32 * q + 4, :, :].rearrange("p g s -> p (g s)").bitcast(I32),
+                scales_picked[32 * q : 32 * q + 32 : 4, :].bitcast(I32),
             )
 
-        load_w1(1, 0, "xs_table")
+        load_first_half(1, "scale_table")
 
-        def gather_words(g, start, stop, tag=None):
-            picked = sb("xw_picked%d_%d" % (g, start), [P, stop - start], U32, tag)
-            nc.vector.tensor_copy(picked[:], xw_table[g][:].bitcast(U32).indirect(entries(offs_sb, start, stop)))
-            xw_picked[g].append((start, stop, picked))
+        words_picked = {}
 
-        def round_w1(dst, g, h, t0):
-            src = w1_raw[g, h].rearrange("p j (m t) -> p m j t", t=4)[:, :, :, t0 : t0 + 2]
-            nc.scalar.copy(dst.rearrange("p t m j -> p m j t"), src)
+        def gather_words(g, tag=None):
+            picked = sbuf_tile("words_picked%d" % g, [P, S], U32, tag)
+            nc.vector.tensor_copy(picked[:], word_table[g][:].bitcast(U32).indirect(offs_sb[:]))
+            words_picked[g] = picked
 
-        def quantize(name, src, width):
-            codes = sb(name + "_codes", [P, width], U32)
-            scales = sb(name + "_scales", [P, width], U8)
-            nc.vector.quantize_mx(out=codes[:].bitcast(FP8X4), scales=scales[:], in_=src)
+        def round_weights(dst, g, half, first_plane, copy=nc.scalar.copy):
+            src = w1_raw[g, half].rearrange("p j (m t) -> p m j t", t=PACK)[:, :, :, first_plane : first_plane + 2]
+            copy(dst.rearrange("p t m j -> p m j t"), src)
+
+        def quantize(name, rounded, width):
+            codes = sbuf_tile(name + "_codes", [P, width], U32)
+            scales = sbuf_tile(name + "_scales", [P, width], U8)
+            nc.vector.quantize_mx(out=codes[:].bitcast(FP8X4), scales=scales[:], in_=rounded)
             return codes, scales
 
-        wq = {}
+        weights = {}
 
-        def early_weights(name, g, h):
-            wb = sb("wb_%s%d" % (name, g), [P, 2, HALF, 4], BF16)
-            round_w1(wb[:], g, h, 0)
-            codes, scales = quantize("w%s%d" % (name, g), wb[:].rearrange("p t m j -> p (t m j)"), P)
-            wq[name, g] = (codes[:], scales[:])
+        def weights_of_half(block, g, half):
+            rounded = sbuf_tile("rounded_%s%d" % (block, g), [P, 2, HALF, PACK], BF16)
+            round_weights(rounded[:], g, half, 0)
+            codes, scales = quantize("w%s%d" % (block, g), rounded[:].rearrange("p t m j -> p (t m j)"), P)
+            weights[block, g] = (codes[:], scales[:])
 
-        wb_late = sb("wb_late", [P, PASSES, 2 * 2 * HALF * 4], BF16)
+        rounded_cd = sbuf_tile("rounded_cd", [P, PASSES, 2 * P * PACK], BF16)
 
-        def late_weights():
-            parts = wb_late[:].rearrange("p g (t h m j) -> p g t h m j", t=2, h=2, j=4)
+        def weights_of_planes_2_and_3():
+            parts = rounded_cd[:].rearrange("p g (t h m j) -> p g t h m j", t=2, h=2, j=PACK)
             for g in range(PASSES):
-                round_w1(parts[:, g, :, 0, :, :], g, 0, 2)
-            nc.scalar.copy(
-                parts[:, :, :, 1, :, :].rearrange("p g t m j -> p g m j t"),
-                w1_second[:].rearrange("p g j (m t) -> p g m j t", t=4)[:, :, :, :, 2:4],
-            )
+                round_weights(parts[:, g, :, 0, :, :], g, 0, 2)
+            round_weights(parts[:, 0, :, 1, :, :], 0, 1, 2, nc.vector.tensor_copy)
+            round_weights(parts[:, 1, :, 1, :, :], 1, 1, 2)
             for g in range(PASSES):
-                codes, scales = quantize("wlate%d" % g, wb_late[:, g, :], 2 * P)
-                wq["B", g] = (codes[:, 0:P], scales[:, 0:P])
-                wq["D", g] = (codes[:, P : 2 * P], scales[:, P : 2 * P])
+                codes, scales = quantize("wCD%d" % g, rounded_cd[:, g, :], 2 * P)
+                weights["C", g] = (codes[:, 0:P], scales[:, 0:P])
+                weights["D", g] = (codes[:, P : 2 * P], scales[:, P : 2 * P])
 
-        def product_pass(acc, name, g, start, stop):
-            codes, scales = wq[name, g]
-            first, picked = [(lo, tile) for lo, hi, tile in xw_picked[g] if lo <= start and stop <= hi][0]
+        def product_pass(acc, block, g, start, stop):
+            codes, scales = weights[block, g]
             nc.tensor.matmul_mx(
-                out=acc,
+                out=acc[:],
                 lhsT=codes.bitcast(FP8X4),
                 lhsT_scale=scales,
-                rhs=picked[:, start - first : stop - first].bitcast(FP8X4),
-                rhs_scale=xs_plane[:, g, start:stop],
+                rhs=words_picked[g][:, start:stop].bitcast(FP8X4),
+                rhs_scale=x_scales_mx[:, g, start:stop],
                 start=(g == 0),
                 stop=(g == PASSES - 1),
             )
 
-        h_sb = {name: sb("h" + name, [P, S], F32) for name in "ACBD"}
+        h = {block: sbuf_tile("h" + block, [P, S], F32) for block in "ABCD"}
 
-        gather_words(0, 0, S)
-        w1_second = sb("w1_second", [P, PASSES, 4, 256], F32, "xw_table0")
+        gather_words(0)
+        w1_second = sbuf_tile("w1_second", [P, PASSES, PACK, H // 2], F32, "word_table0")
         for g in range(PASSES):
             w1_raw[g, 1] = w1_second[:, g, :, :]
-            nc.sync.dma_start(w1_raw[g, 1], w1_view[g, 1])
-        CUT = 768
-        gather_words(1, 0, CUT)
-        early_weights("A", 0, 0)
-        gather_words(1, CUT, S, "wb_A0")
-        pieces = [(start, start + 256) for start in range(0, S, 256)]
-        acc_a = [bank(i, 256) for i in range(4)]
-        for acc, (start, stop) in zip(acc_a, pieces):
-            product_pass(acc[:], "A", 0, start, stop)
-        early_weights("A", 1, 0)
-        for acc, (start, stop), copy in zip(acc_a, pieces, (nc.vector.tensor_copy, nc.scalar.copy, nc.vector.tensor_copy, nc.vector.tensor_copy)):
-            product_pass(acc[:], "A", 1, start, stop)
-            copy(h_sb["A"][:, start:stop], acc[:])
+            nc.sync.dma_start(w1_raw[g, 1], w1_parts[g, 1])
+        weights_of_half("A", 0, 0)
+        gather_words(1, "rounded_A0")
 
-        w2s = sb("w2s", [P, N], U8, tag="xw_table1")
-        nc.vector.memset(w2s[:].bitcast(I32), 0)
+        pieces_a = ((0, 256, nc.scalar.copy), (256, BANK, nc.vector.tensor_copy), (BANK, S, nc.vector.tensor_copy))
+        acc_a = [psum_bank(index, stop - start) for index, (start, stop, copy) in enumerate(pieces_a)]
+        for acc, (start, stop, copy) in zip(acc_a, pieces_a):
+            product_pass(acc, "A", 0, start, stop)
+        weights_of_half("A", 1, 0)
+        for acc, (start, stop, copy) in zip(acc_a, pieces_a):
+            product_pass(acc, "A", 1, start, stop)
+            copy(h["A"][:, start:stop], acc[:])
+
+        w2_codes = sbuf_tile("w2_codes", [P, 2 * N], U8, tag="rounded_A1")
+        nc.sync.dma_start(w2_codes[:].bitcast(I32), w2_words[0].bitcast(I32))
+        w2_scales_mx = sbuf_tile("w2_scales_mx", [P, N], U8, tag="word_table1")
+        nc.gpsimd.memset(w2_scales_mx[:].bitcast(I32), 0)
         for q in range(4):
             nc.sync.dma_start(
-                w2s[32 * q : 32 * q + 4, :].bitcast(I32), w2_scales[0, 4 * q : 4 * q + 4, :].bitcast(I32)
+                w2_scales_mx[32 * q : 32 * q + 4, :].bitcast(I32), w2_scales[0, 4 * q : 4 * q + 4, :].bitcast(I32)
             )
 
-        def project(index, name, start, stop):
-            acc = bank(index, stop - start)
-            cuts = [start] + [c for c in (CUT,) if start < c < stop] + [stop]
-            for lo, hi in zip(cuts, cuts[1:]):
-                for g in range(PASSES):
-                    product_pass(acc[:, lo - start : hi - start], name, g, lo, hi)
-            nc.scalar.copy(h_sb[name][:, start:stop], acc[:])
+        def project(bank, block, start, stop):
+            acc = psum_bank(bank, stop - start)
+            for g in range(PASSES):
+                product_pass(acc, block, g, start, stop)
+            nc.scalar.copy(h[block][:, start:stop], acc[:])
 
         for g in range(PASSES):
-            early_weights("C", g, 1)
-        project(4, "C", 0, 512)
-        project(5, "C", 512, S)
-        late_weights()
-        for index, name, start, stop in ((6, "B", 0, 512), (7, "D", 0, 512), (0, "D", 512, 768), (1, "B", 512, S), (2, "D", 768, S)):
-            project(index, name, start, stop)
+            weights_of_half("B", g, 1)
+        project(4, "B", 0, BANK)
+        project(5, "B", BANK, S)
+        weights_of_planes_2_and_3()
+        project(6, "C", 0, BANK)
+        project(7, "D", 0, BANK)
+        project(3, "D", BANK, 768)
+        project(0, "C", BANK, S)
+        project(1, "D", 768, S)
 
-        CH = 128
+        def gather_left(dst, block, start, stop):
+            nc.vector.tensor_copy(dst, h[block][:].indirect(entries(left_sb, start, stop)))
 
-        def gather_left(name, start, stop, tag=None):
-            picked = sb("left_%s%d" % (name, start), [P, stop - start], F32, tag)
-            nc.vector.tensor_copy(picked[:], h_sb[name][:].indirect(entries(left_sb, start, stop)))
-            return picked
+        def right_minus_left(dst, block, start, stop, left_values):
+            nc.vector.tensor_tensor(dst, h[block][:].indirect(entries(right_sb, start, stop)), left_values, SUB)
 
-        def subtract_right(dst, name, start, stop, picked):
-            nc.vector.tensor_tensor(dst, h_sb[name][:].indirect(entries(right_sb, start, stop)), picked, SUB)
+        diff_second = sbuf_tile("diff_second", [P, 2, PACK, V // 4], F32)
+        diff_first = sbuf_tile("diff_first", [P, PACK, V // 2], F32)
+        diff = [diff_first[:], diff_second[:, 0, :, :], diff_second[:, 1, :, :]]
 
-        late = sb("diff_late", [P, 2, 4, CH], F32)
-        early = sb("diff_early", [P, 4, 2 * CH], F32)
-        diff = {0: early[:], 256: late[:, 0, :, :], 384: late[:, 1, :, :]}
-
-        def move_rows(dst_rows, d, start):
+        def move_first_half(partitions, block_diff):
             for t in range(2):
-                src = d[HALF * t : HALF * (t + 1), start : start + 2 * CH]
-                if start == 0:
-                    nc.sync.dma_start(early[dst_rows, t, :], src)
-                else:
-                    nc.sync.dma_start(late[dst_rows, :, t, :], src.rearrange("p (c v) -> p c v", v=CH))
+                nc.sync.dma_start(diff_first[partitions, t, :], block_diff[HALF * t : HALF * (t + 1), 0 : V // 2])
 
-        d_a = wb_late[:, 0, :].bitcast(F32)
-        subtract_right(d_a, "A", 0, V, gather_left("A", 0, V, "wb_C1")[:])
-        for start in (0, V // 2):
-            move_rows(slice(0, HALF), d_a, start)
-        d_c = sb("d_c", [P, V], F32)
-        halves = [(0, V // 2), (V // 2, V)]
-        left_c = [gather_left("C", start, stop) for start, stop in halves]
-        for picked, (start, stop) in zip(left_c, halves):
-            subtract_right(d_c[:, start:stop], "C", start, stop, picked[:])
-            move_rows(slice(HALF, P), d_c[:], start)
+        def move_second_half(partitions, block_diff):
+            for t in range(2):
+                nc.sync.dma_start(
+                    diff_second[partitions, :, t, :],
+                    block_diff[HALF * t : HALF * (t + 1), V // 2 : V].rearrange("p (c v) -> p c v", c=2),
+                )
 
-        zb = [sb("zb%d" % i, [P, width, 4], BF16) for i, width in enumerate((256, 128, 128))]
+        diff_a = sbuf_tile("diff_a", [P, V], F32)
+        left_a = sbuf_tile("left_a", [P, V], F32, "rounded_B1")
+        gather_left(left_a[:], "A", 0, V)
+        right_minus_left(diff_a[:], "A", 0, V, left_a[:])
+        move_first_half(slice(0, HALF), diff_a)
+        move_second_half(slice(0, HALF), diff_a)
 
-        def take_abs(index, start):
+        diff_b = sbuf_tile("diff_b", [P, V], F32)
+        left_b = []
+        for start, stop in PAIR_HALVES:
+            left_b.append(sbuf_tile("left_b%d" % start, [P, stop - start], F32))
+            gather_left(left_b[-1][:], "B", start, stop)
+        for left_values, (start, stop), move in zip(left_b, PAIR_HALVES, (move_first_half, move_second_half)):
+            right_minus_left(diff_b[:, start:stop], "B", start, stop, left_values[:])
+            move(slice(HALF, P), diff_b)
+
+        z_rounded = [sbuf_tile("z_rounded%d" % a, [P, b - a, PACK], BF16) for a, b in CHUNKS]
+
+        def take_abs(chunk):
             nc.scalar.activation(
-                zb[index][:].rearrange("p (c i) t -> p c t i", i=4),
-                diff[start].rearrange("p t (c i) -> p c t i", i=4),
+                z_rounded[chunk][:].rearrange("p (c i) t -> p c t i", i=4),
+                diff[chunk].rearrange("p t (c i) -> p c t i", i=4),
                 ABS,
             )
 
-        def finish(index, a, cuts, copy):
-            n = cuts[-1]
-            codes = sb("z_codes%d" % index, [P, n], U32)
-            scales = sb("z_scales%d" % index, [P, n], U8)
-            for lo, hi in zip([0] + cuts, cuts):
-                nc.vector.quantize_mx(
-                    out=codes[:, lo:hi].bitcast(FP8X4),
-                    scales=scales[:, lo:hi],
-                    in_=zb[index][:, lo:hi, :].rearrange("p v t -> p (v t)"),
-                )
-            acc = bank(3 + index, n)
+        plane = {"C": 2, "D": 3}
+        lefts = ctx.enter_context(tc.tile_pool(name="lefts", bufs=2))
+        for blocks, (first, last), chunks in zip(("CD", "DC"), PAIR_HALVES, ((0,), (1, 2))):
+            left_of = {}
+            for block in blocks:
+                left_of[block] = lefts.tile([P, last - first], F32, name="left_%s%d" % (block, first), tag="left")
+                gather_left(left_of[block][:], block, first, last)
+            for chunk in chunks:
+                start, stop = CHUNKS[chunk]
+                for block in blocks:
+                    left_values = left_of[block][:, start - first : stop - first]
+                    right_minus_left(diff[chunk][:, plane[block], :], block, start, stop, left_values)
+                take_abs(chunk)
+
+        def second_product(chunk, bank, copy):
+            start, stop = CHUNKS[chunk]
+            codes, scales = quantize("z%d" % chunk, z_rounded[chunk][:].rearrange("p v t -> p (v t)"), stop - start)
+            acc = psum_bank(bank, stop - start)
             nc.tensor.matmul_mx(
                 out=acc[:],
-                lhsT=w2w[:].bitcast(FP4X4),
-                lhsT_scale=w2s[:],
+                lhsT=w2_codes[:].bitcast(FP4X4),
+                lhsT_scale=w2_scales_mx[:],
                 rhs=codes[:].bitcast(FP8X4),
                 rhs_scale=scales[:],
                 start=True,
                 stop=True,
             )
-            res = sb("res%d" % index, [P, n], F32)
-            copy(res[:], acc[:])
-            nc.sync.dma_start(out[:, a : a + n], res[:])
+            result = sbuf_tile("result%d" % chunk, [P, stop - start], F32)
+            copy(result[:], acc[:])
+            nc.sync.dma_start(out[:, start:stop], result[:])
 
-        plane = {"B": 2, "D": 3}
-        lefts = ctx.enter_context(tc.tile_pool(name="lefts", bufs=2))
-        for names, a, cuts in (("BD", 0, (256,)), ("DB", 256, (384, 512))):
-            picked = {}
-            for name in names:
-                picked[name] = lefts.tile([P, cuts[-1] - a], F32, name="left_%s%d" % (name, a), tag="left")
-                nc.vector.tensor_copy(picked[name][:], h_sb[name][:].indirect(entries(left_sb, a, cuts[-1])))
-            for lo, hi in zip((a,) + cuts, cuts):
-                for name in names:
-                    subtract_right(
-                        diff[lo][:, plane[name], :],
-                        name, lo, hi, picked[name][:, lo - a : hi - a],
-                    )
-                take_abs((0, 256, 384).index(lo), lo)
-        finish(0, 0, [256], nc.scalar.copy)
-        finish(1, 256, [128], nc.scalar.copy)
-        finish(2, 384, [128], nc.vector.tensor_copy)
+        second_product(0, 2, nc.scalar.copy)
+        second_product(1, 4, nc.scalar.copy)
+        second_product(2, 5, nc.vector.tensor_copy)

@@ -55,25 +55,27 @@ def tile_picked_phpair_abs_p_kernel(
         w1_parts = w1.rearrange("(g p j) (h c) -> g h p j c", g=PASSES, j=PACK, h=2)
         w1_raw = {}
 
-        def load_words(g):
-            nc.sync.dma_start(word_table[g][:], x_words[g].rearrange("p n t -> p (n t)").bitcast(I32))
+        def load_words(g, start, stop):
+            words = x_words[g].rearrange("p n t -> p (n t)").bitcast(I32)
+            nc.sync.dma_start(word_table[g][:, start:stop], words[:, start:stop])
 
-        def load_first_half(g, tag=None):
-            raw = sbuf_tile("w1_first%d" % g, [P, PACK, H // 2], F32, tag)
-            w1_raw[g, 0] = raw[:]
-            nc.sync.dma_start(raw[:], w1_parts[g, 0])
+        def load_weights(dst, g, half):
+            w1_raw[g, half] = dst
+            nc.sync.dma_start(dst, w1_parts[g, half])
 
         nc.vector.memset(scale_table[:, 0:ZEROED_BY_VECTOR].bitcast(I32), 0)
         nc.gpsimd.memset(scale_table[:, ZEROED_BY_VECTOR:T].bitcast(I32), 0)
         nc.vector.memset(x_scales_mx[:].rearrange("p g s -> p (g s)").bitcast(I32), 0)
 
         nc.sync.dma_start(offs_sb[:], offs)
+        load_words(0, 0, T // 4)
         nc.sync.dma_start(left_sb[:], left)
         nc.sync.dma_start(right_sb[:], right)
         nc.sync.dma_start(scale_table[0:P:4, :].bitcast(I32), x_scales.rearrange("z r c -> r z c").bitcast(I32))
-        load_words(0)
-        load_first_half(0)
-        load_words(1)
+        load_words(0, T // 4, T)
+        w1_first = sbuf_tile("w1_first", [P, PACK, H // 2], F32)
+        load_weights(w1_first[:], 0, 0)
+        load_words(1, 0, T)
 
         nc.vector.tensor_copy(scales_picked[:], scale_table[:].indirect(offs_sb[:]))
         for q in range(4):
@@ -82,7 +84,9 @@ def tile_picked_phpair_abs_p_kernel(
                 scales_picked[32 * q : 32 * q + 32 : 4, :].bitcast(I32),
             )
 
-        load_first_half(1, "scale_table")
+        w1_rest = sbuf_tile("w1_rest", [P, 3, PACK, H // 2], F32, "scale_table")
+        for slot, (g, half) in enumerate(((1, 0), (0, 1), (1, 1))):
+            load_weights(w1_rest[:, slot, :, :], g, half)
 
         words_picked = {}
 
@@ -137,10 +141,6 @@ def tile_picked_phpair_abs_p_kernel(
         h = {block: sbuf_tile("h" + block, [P, S], F32) for block in "ABCD"}
 
         gather_words(0)
-        w1_second = sbuf_tile("w1_second", [P, PASSES, PACK, H // 2], F32, "word_table0")
-        for g in range(PASSES):
-            w1_raw[g, 1] = w1_second[:, g, :, :]
-            nc.sync.dma_start(w1_raw[g, 1], w1_parts[g, 1])
         weights_of_half("A", 0, 0)
         gather_words(1, "rounded_A0")
 
@@ -148,6 +148,17 @@ def tile_picked_phpair_abs_p_kernel(
         acc_a = [psum_bank(index, stop - start) for index, (start, stop, copy) in enumerate(pieces_a)]
         for acc, (start, stop, copy) in zip(acc_a, pieces_a):
             product_pass(acc, "A", 0, start, stop)
+        unread = psum_bank(7, BANK)
+        for start in (0, BANK):
+            nc.tensor.matmul_mx(
+                out=unread[:],
+                lhsT=weights["A", 0][0].bitcast(FP8X4),
+                lhsT_scale=weights["A", 0][1],
+                rhs=words_picked[0][:, start : start + BANK].bitcast(FP8X4),
+                rhs_scale=x_scales_mx[:, 0, start : start + BANK],
+                start=True,
+                stop=True,
+            )
         weights_of_half("A", 1, 0)
         for acc, (start, stop, copy) in zip(acc_a, pieces_a):
             product_pass(acc, "A", 1, start, stop)

@@ -14,6 +14,7 @@ U8 = mybir.dt.uint8
 FP8X4 = mybir.dt.float8_e4m3fn_x4
 FP4X4 = mybir.dt.float4_e2m1fn_x4
 ABS = mybir.ActivationFunctionType.Abs
+COPY = mybir.ActivationFunctionType.Copy
 SUB = mybir.AluOpType.subtract
 
 P = 128
@@ -237,12 +238,11 @@ def tile_picked_phpair_abs_p_kernel(
             )
 
         plane = {"C": 2, "D": 3}
-        lefts = ctx.enter_context(tc.tile_pool(name="lefts", bufs=2))
         for blocks, (first, last), chunks in zip(("CD", "DC"), PAIR_HALVES, ((0,), (1, 2))):
             left_of = {}
             for block in blocks:
-                left_of[block] = lefts.tile([P, last - first], F32, name="left_%s%d" % (block, first), tag="left")
-                gather_left(left_of[block][:], block, first, last)
+                left_of[block] = sbuf_tile("left_%s%d" % (block, first), [P, last - first], F32)
+                nc.scalar.activation(left_of[block][:], h[block][:].indirect(entries(left_sb, first, last)), COPY)
             for chunk in chunks:
                 start, stop = CHUNKS[chunk]
                 for block in blocks:

@@ -25,7 +25,9 @@ STRIPE = 16
 BANK = 512
 ZEROED_BY_VECTOR = 1216
 PAIR_HALVES = ((0, V // 2), (V // 2, V))
-CHUNKS = ((0, 256), (256, 384), (384, 512))
+PRODUCTS = ((0, 256), (256, 384), (384, 512))
+CHUNK = 128
+CUT = 768
 
 
 def tile_picked_phpair_abs_p_kernel(
@@ -74,9 +76,9 @@ def tile_picked_phpair_abs_p_kernel(
         nc.sync.dma_start(right_sb[:], right)
         nc.sync.dma_start(scale_table[0:P:4, :].bitcast(I32), x_scales.rearrange("z r c -> r z c").bitcast(I32))
         load_words(0, T // 4, T)
+        load_words(1, 0, T)
         w1_first = sbuf_tile("w1_first", [P, PACK, H // 2], F32)
         load_weights(w1_first[:], 0, 0)
-        load_words(1, 0, T)
 
         nc.vector.tensor_copy(scales_picked[:], scale_table[:].indirect(offs_sb[:]))
         for q in range(4):
@@ -89,14 +91,18 @@ def tile_picked_phpair_abs_p_kernel(
         for slot, (g, half) in enumerate(((1, 0), (0, 1), (1, 1))):
             load_weights(w1_rest[:, slot, :, :], g, half)
 
-        words_picked = {}
+        picked = {}
 
-        def gather_words(g, tag=None):
-            picked = sbuf_tile("words_picked%d" % g, [P, S], U32, tag)
-            nc.vector.tensor_copy(picked[:], word_table[g][:].bitcast(U32).indirect(offs_sb[:]))
-            words_picked[g] = picked
+        def gather_words(g, start, stop, tag=None):
+            words = sbuf_tile("words_picked%d_%d" % (g, start), [P, stop - start], U32, tag)
+            nc.vector.tensor_copy(words[:], word_table[g][:].bitcast(U32).indirect(entries(offs_sb, start, stop)))
+            picked[g, start] = words
 
-        def round_weights(dst, g, half, first_plane, copy=nc.scalar.copy):
+        def picked_words(g, start, stop):
+            first = max(key[1] for key in picked if key[0] == g and key[1] <= start)
+            return picked[g, first][:, start - first : stop - first]
+
+        def round_weights(dst, g, half, first_plane, copy):
             src = w1_raw[g, half].rearrange("p j (m t) -> p m j t", t=PACK)[:, :, :, first_plane : first_plane + 2]
             copy(dst.rearrange("p t m j -> p m j t"), src)
 
@@ -107,65 +113,80 @@ def tile_picked_phpair_abs_p_kernel(
             return codes, scales
 
         weights = {}
+        rounded = {}
 
-        def weights_of_half(block, g, half):
-            rounded = sbuf_tile("rounded_%s%d" % (block, g), [P, 2, HALF, PACK], BF16)
-            round_weights(rounded[:], g, half, 0)
-            codes, scales = quantize("w%s%d" % (block, g), rounded[:].rearrange("p t m j -> p (t m j)"), P)
+        def round_half(block, g, half, copy):
+            rounded[block, g] = sbuf_tile("rounded_%s%d" % (block, g), [P, 2, HALF, PACK], BF16)
+            round_weights(rounded[block, g][:], g, half, 0, copy)
+
+        def quantize_half(block, g):
+            codes, scales = quantize("w%s%d" % (block, g), rounded[block, g][:].rearrange("p t m j -> p (t m j)"), P)
             weights[block, g] = (codes[:], scales[:])
 
-        rounded_cd = sbuf_tile("rounded_cd", [P, PASSES, 2 * P * PACK], BF16)
+        rounded_cd = [sbuf_tile("rounded_cd%d" % g, [P, 2, 2, HALF, PACK], BF16) for g in range(PASSES)]
 
-        def weights_of_planes_2_and_3():
-            parts = rounded_cd[:].rearrange("p g (t h m j) -> p g t h m j", t=2, h=2, j=PACK)
-            for g in range(PASSES):
-                round_weights(parts[:, g, :, 0, :, :], g, 0, 2)
-            round_weights(parts[:, 0, :, 1, :, :], 0, 1, 2, nc.vector.tensor_copy)
-            round_weights(parts[:, 1, :, 1, :, :], 1, 1, 2)
-            for g in range(PASSES):
-                codes, scales = quantize("wCD%d" % g, rounded_cd[:, g, :], 2 * P)
-                weights["C", g] = (codes[:, 0:P], scales[:, 0:P])
-                weights["D", g] = (codes[:, P : 2 * P], scales[:, P : 2 * P])
+        def round_cd(g, half, copy):
+            round_weights(rounded_cd[g][:, :, half, :, :], g, half, 2, copy)
 
-        def product_pass(acc, block, g, start, stop):
+        def quantize_cd(g):
+            codes, scales = quantize("wCD%d" % g, rounded_cd[g][:].rearrange("p t h m j -> p (t h m j)"), 2 * P)
+            weights["C", g] = (codes[:, 0:P], scales[:, 0:P])
+            weights["D", g] = (codes[:, P : 2 * P], scales[:, P : 2 * P])
+
+        def product_pass(acc, block, g, start, stop, last):
             codes, scales = weights[block, g]
             nc.tensor.matmul_mx(
                 out=acc[:],
                 lhsT=codes.bitcast(FP8X4),
                 lhsT_scale=scales,
-                rhs=words_picked[g][:, start:stop].bitcast(FP8X4),
+                rhs=picked_words(g, start, stop).bitcast(FP8X4),
                 rhs_scale=x_scales_mx[:, g, start:stop],
                 start=(g == 0),
-                stop=(g == PASSES - 1),
+                stop=last,
             )
 
-        h = {block: sbuf_tile("h" + block, [P, S], F32) for block in "ABCD"}
+        h = {block: sbuf_tile("h" + block, [P, S], F32) for block in "AB"}
 
-        gather_words(0)
-        weights_of_half("A", 0, 0)
-        gather_words(1, "rounded_A0")
-
-        pieces_a = ((0, 256, nc.scalar.copy), (256, BANK, nc.vector.tensor_copy), (BANK, S, nc.vector.tensor_copy))
-        acc_a = [psum_bank(index, stop - start) for index, (start, stop, copy) in enumerate(pieces_a)]
-        for acc, (start, stop, copy) in zip(acc_a, pieces_a):
-            product_pass(acc, "A", 0, start, stop)
+        gather_words(0, 0, S)
         unread = psum_bank(7, BANK)
         for start in (0, BANK):
             nc.tensor.matmul_mx(
                 out=unread[:],
-                lhsT=weights["A", 0][0].bitcast(FP8X4),
-                lhsT_scale=weights["A", 0][1],
-                rhs=words_picked[0][:, start : start + BANK].bitcast(FP8X4),
+                lhsT=picked_words(0, 0, P).bitcast(FP8X4),
+                lhsT_scale=x_scales_mx[:, 0, 0:P],
+                rhs=picked_words(0, start, start + BANK).bitcast(FP8X4),
                 rhs_scale=x_scales_mx[:, 0, start : start + BANK],
                 start=True,
                 stop=True,
             )
-        weights_of_half("A", 1, 0)
-        for acc, (start, stop, copy) in zip(acc_a, pieces_a):
-            product_pass(acc, "A", 1, start, stop)
-            copy(h["A"][:, start:stop], acc[:])
+        gather_words(1, 0, CUT)
+        round_half("A", 0, 0, nc.scalar.copy)
+        quantize_half("A", 0)
+        round_cd(0, 0, nc.scalar.copy)
+        round_half("A", 1, 0, nc.scalar.copy)
+        quantize_half("A", 1)
+        gather_words(1, CUT, S, "rounded_A1")
+        round_cd(1, 0, nc.scalar.copy)
+        round_half("B", 0, 1, nc.scalar.copy)
 
-        w2_codes = sbuf_tile("w2_codes", [P, 2 * N], U8, tag="rounded_A1")
+        accs = {}
+
+        def products(block, first_bank):
+            accs[block] = [psum_bank(first_bank + index, BANK) for index in range(2)]
+            for index in range(2):
+                product_pass(accs[block][index], block, 0, index * BANK, (index + 1) * BANK, False)
+            product_pass(accs[block][0], block, 1, 0, BANK, True)
+            product_pass(accs[block][1][:, 0 : CUT - BANK], block, 1, BANK, CUT, False)
+            product_pass(accs[block][1][:, CUT - BANK : BANK], block, 1, CUT, S, True)
+
+        def empty(block, index, copy):
+            copy(h[block][:, index * BANK : (index + 1) * BANK], accs[block][index][:])
+
+        products("A", 0)
+        for index in range(2):
+            empty("A", index, nc.scalar.copy)
+
+        w2_codes = sbuf_tile("w2_codes", [P, 2 * N], U8, tag="word_table0")
         nc.sync.dma_start(w2_codes[:].bitcast(I32), w2_words[0].bitcast(I32))
         w2_scales_mx = sbuf_tile("w2_scales_mx", [P, N], U8, tag="word_table1")
         nc.gpsimd.memset(w2_scales_mx[:].bitcast(I32), 0)
@@ -174,85 +195,89 @@ def tile_picked_phpair_abs_p_kernel(
                 w2_scales_mx[32 * q : 32 * q + 4, :].bitcast(I32), w2_scales[0, 4 * q : 4 * q + 4, :].bitcast(I32)
             )
 
-        def project(bank, block, start, stop):
-            acc = psum_bank(bank, stop - start)
-            for g in range(PASSES):
-                product_pass(acc, block, g, start, stop)
-            nc.scalar.copy(h[block][:, start:stop], acc[:])
+        round_cd(0, 1, nc.vector.tensor_copy)
+        quantize_half("B", 0)
+        round_half("B", 1, 1, nc.vector.tensor_copy)
+        round_cd(1, 1, nc.vector.tensor_copy)
+        quantize_half("B", 1)
+        quantize_cd(0)
+        quantize_cd(1)
+        products("B", 2)
+        products("C", 0)
 
-        for g in range(PASSES):
-            weights_of_half("B", g, 1)
-        project(4, "B", 0, BANK)
-        project(5, "B", BANK, S)
-        weights_of_planes_2_and_3()
-        project(6, "C", 0, BANK)
-        project(7, "D", 0, BANK)
-        project(3, "D", BANK, 768)
-        project(0, "C", BANK, S)
-        project(1, "D", 768, S)
-
-        def gather_left(dst, block, start, stop):
-            nc.vector.tensor_copy(dst, h[block][:].indirect(entries(left_sb, start, stop)))
+        def gather_left(block, start, stop, on_scalar=True):
+            left_values = sbuf_tile("left_%s%d" % (block, start), [P, stop - start], F32)
+            window = h[block][:].indirect(entries(left_sb, start, stop))
+            if on_scalar:
+                nc.scalar.activation(left_values[:], window, COPY)
+            else:
+                nc.vector.tensor_copy(left_values[:], window)
+            return left_values
 
         def right_minus_left(dst, block, start, stop, left_values):
             nc.vector.tensor_tensor(dst, h[block][:].indirect(entries(right_sb, start, stop)), left_values, SUB)
 
-        diff_second = sbuf_tile("diff_second", [P, 2, PACK, V // 4], F32)
-        diff_first = sbuf_tile("diff_first", [P, PACK, V // 2], F32)
-        diff = [diff_first[:], diff_second[:, 0, :, :], diff_second[:, 1, :, :]]
+        diff = [sbuf_tile("diff%d" % half, [P, 2, PACK, CHUNK], F32) for half in range(2)]
 
-        def move_first_half(partitions, block_diff):
-            for t in range(2):
-                nc.sync.dma_start(diff_first[partitions, t, :], block_diff[HALF * t : HALF * (t + 1), 0 : V // 2])
-
-        def move_second_half(partitions, block_diff):
+        def move(partitions, block_diff, half):
+            start, stop = PAIR_HALVES[half]
             for t in range(2):
                 nc.sync.dma_start(
-                    diff_second[partitions, :, t, :],
-                    block_diff[HALF * t : HALF * (t + 1), V // 2 : V].rearrange("p (c v) -> p c v", c=2),
+                    diff[half][partitions, :, t, :],
+                    block_diff[HALF * t : HALF * (t + 1), start:stop].rearrange("p (c v) -> p c v", c=2),
                 )
 
-        diff_a = sbuf_tile("diff_a", [P, V], F32)
-        left_a = sbuf_tile("left_a", [P, V], F32, "rounded_B1")
-        gather_left(left_a[:], "A", 0, V)
+        left_a = gather_left("A", 0, V)
+        empty("B", 0, nc.vector.tensor_copy)
+        empty("B", 1, nc.scalar.copy)
+        products("D", 2)
+        diff_a = sbuf_tile("diff_a", [P, V], F32, "wB1_codes")
         right_minus_left(diff_a[:], "A", 0, V, left_a[:])
-        move_first_half(slice(0, HALF), diff_a)
-        move_second_half(slice(0, HALF), diff_a)
+        for half in range(2):
+            move(slice(0, HALF), diff_a, half)
 
         diff_b = sbuf_tile("diff_b", [P, V], F32)
-        left_b = []
-        for start, stop in PAIR_HALVES:
-            left_b.append(sbuf_tile("left_b%d" % start, [P, stop - start], F32))
-            gather_left(left_b[-1][:], "B", start, stop)
-        for left_values, (start, stop), move in zip(left_b, PAIR_HALVES, (move_first_half, move_second_half)):
-            right_minus_left(diff_b[:, start:stop], "B", start, stop, left_values[:])
-            move(slice(HALF, P), diff_b)
+        for half, (start, stop) in enumerate(PAIR_HALVES):
+            right_minus_left(diff_b[:, start:stop], "B", start, stop, gather_left("B", start, stop)[:])
+            move(slice(HALF, P), diff_b, half)
+        h["C"] = sbuf_tile("hC", [P, S], F32, "left_A0")
+        for index in range(2):
+            empty("C", index, nc.scalar.copy)
 
-        z_rounded = [sbuf_tile("z_rounded%d" % a, [P, b - a, PACK], BF16) for a, b in CHUNKS]
+        h["D"] = sbuf_tile("hD", [P, S], F32, "left_B0")
+        empty("D", 0, nc.scalar.copy)
+        empty("D", 1, nc.vector.tensor_copy)
+
+        left_of = {}
+        left_of["C", 0] = gather_left("C", 0, V // 2)
+        left_of["D", 0] = gather_left("D", 0, V // 2)
+        left_of["C", 1] = gather_left("C", V // 2, V)
+        left_of["D", 1] = gather_left("D", V // 2, V, on_scalar=False)
+
+        z_rounded = [sbuf_tile("z_rounded%d" % a, [P, b - a, PACK], BF16) for a, b in PRODUCTS]
 
         def take_abs(chunk):
+            first = chunk * CHUNK
+            part = max(index for index, (a, b) in enumerate(PRODUCTS) if a <= first)
+            offset = first - PRODUCTS[part][0]
             nc.scalar.activation(
-                z_rounded[chunk][:].rearrange("p (c i) t -> p c t i", i=4),
-                diff[chunk].rearrange("p t (c i) -> p c t i", i=4),
+                z_rounded[part][:, offset : offset + CHUNK, :].rearrange("p (c i) t -> p c t i", i=4),
+                diff[chunk // 2][:, chunk % 2, :, :].rearrange("p t (c i) -> p c t i", i=4),
                 ABS,
             )
 
         plane = {"C": 2, "D": 3}
-        for blocks, (first, last), chunks in zip(("CD", "DC"), PAIR_HALVES, ((0,), (1, 2))):
-            left_of = {}
-            for block in blocks:
-                left_of[block] = sbuf_tile("left_%s%d" % (block, first), [P, last - first], F32)
-                nc.scalar.activation(left_of[block][:], h[block][:].indirect(entries(left_sb, first, last)), COPY)
-            for chunk in chunks:
-                start, stop = CHUNKS[chunk]
-                for block in blocks:
-                    left_values = left_of[block][:, start - first : stop - first]
-                    right_minus_left(diff[chunk][:, plane[block], :], block, start, stop, left_values)
-                take_abs(chunk)
+        for chunk in range(V // CHUNK):
+            half, inner = divmod(chunk, 2)
+            for block in "CD":
+                left_values = left_of[block, half][:, inner * CHUNK : (inner + 1) * CHUNK]
+                dst = diff[half][:, inner, plane[block], :]
+                right_minus_left(dst, block, chunk * CHUNK, (chunk + 1) * CHUNK, left_values)
+            take_abs(chunk)
 
-        def second_product(chunk, bank, copy):
-            start, stop = CHUNKS[chunk]
-            codes, scales = quantize("z%d" % chunk, z_rounded[chunk][:].rearrange("p v t -> p (v t)"), stop - start)
+        def second_product(part, bank, copy):
+            start, stop = PRODUCTS[part]
+            codes, scales = quantize("z%d" % part, z_rounded[part][:].rearrange("p v t -> p (v t)"), stop - start)
             acc = psum_bank(bank, stop - start)
             nc.tensor.matmul_mx(
                 out=acc[:],
@@ -263,10 +288,10 @@ def tile_picked_phpair_abs_p_kernel(
                 start=True,
                 stop=True,
             )
-            result = sbuf_tile("result%d" % chunk, [P, stop - start], F32)
+            result = sbuf_tile("result%d" % part, [P, stop - start], F32)
             copy(result[:], acc[:])
             nc.sync.dma_start(out[:, start:stop], result[:])
 
-        second_product(0, 2, nc.scalar.copy)
-        second_product(1, 4, nc.scalar.copy)
-        second_product(2, 5, nc.vector.tensor_copy)
+        second_product(0, 4, nc.scalar.copy)
+        second_product(1, 5, nc.scalar.copy)
+        second_product(2, 6, nc.vector.tensor_copy)

@@ -72,8 +72,6 @@ def tile_picked_phpair_abs_p_kernel(
 
         nc.sync.dma_start(offs_sb[:], offs)
         load_words(0, 0, T // 4)
-        nc.sync.dma_start(left_sb[:], left)
-        nc.sync.dma_start(right_sb[:], right)
         nc.sync.dma_start(scale_table[0:P:4, :].bitcast(I32), x_scales.rearrange("z r c -> r z c").bitcast(I32))
         load_words(0, T // 4, T)
         load_words(1, 0, T)
@@ -90,6 +88,8 @@ def tile_picked_phpair_abs_p_kernel(
         w1_rest = sbuf_tile("w1_rest", [P, 3, PACK, H // 2], F32, "scale_table")
         for slot, (g, half) in enumerate(((1, 0), (0, 1), (1, 1))):
             load_weights(w1_rest[:, slot, :, :], g, half)
+        nc.sync.dma_start(left_sb[:], left)
+        nc.sync.dma_start(right_sb[:], right)
 
         picked = {}
 
@@ -106,8 +106,8 @@ def tile_picked_phpair_abs_p_kernel(
             src = w1_raw[g, half].rearrange("p j (m t) -> p m j t", t=PACK)[:, :, :, first_plane : first_plane + 2]
             copy(dst.rearrange("p t m j -> p m j t"), src)
 
-        def quantize(name, rounded, width):
-            codes = sbuf_tile(name + "_codes", [P, width], U32)
+        def quantize(name, rounded, width, tag=None):
+            codes = sbuf_tile(name + "_codes", [P, width], U32, tag)
             scales = sbuf_tile(name + "_scales", [P, width], U8)
             nc.vector.quantize_mx(out=codes[:].bitcast(FP8X4), scales=scales[:], in_=rounded)
             return codes, scales
@@ -128,8 +128,9 @@ def tile_picked_phpair_abs_p_kernel(
         def round_cd(g, half, copy):
             round_weights(rounded_cd[g][:, :, half, :, :], g, half, 2, copy)
 
-        def quantize_cd(g):
-            codes, scales = quantize("wCD%d" % g, rounded_cd[g][:].rearrange("p t h m j -> p (t h m j)"), 2 * P)
+        def quantize_cd(g, tag=None):
+            flat = rounded_cd[g][:].rearrange("p t h m j -> p (t h m j)")
+            codes, scales = quantize("wCD%d" % g, flat, 2 * P, tag)
             weights["C", g] = (codes[:, 0:P], scales[:, 0:P])
             weights["D", g] = (codes[:, P : 2 * P], scales[:, P : 2 * P])
 
@@ -145,7 +146,7 @@ def tile_picked_phpair_abs_p_kernel(
                 stop=last,
             )
 
-        h = {block: sbuf_tile("h" + block, [P, S], F32) for block in "AB"}
+        h = {block: sbuf_tile("h" + block, [P, S], F32) for block in "ABC"}
 
         gather_words(0, 0, S)
         unread = psum_bank(7, BANK)
@@ -200,10 +201,10 @@ def tile_picked_phpair_abs_p_kernel(
         round_half("B", 1, 1, nc.vector.tensor_copy)
         round_cd(1, 1, nc.vector.tensor_copy)
         quantize_half("B", 1)
-        quantize_cd(0)
+        quantize_cd(0, "rounded_B1")
         quantize_cd(1)
-        products("B", 2)
-        products("C", 0)
+        for n, block in enumerate("BCD"):
+            products(block, 2 * n + 2)
 
         def gather_left(block, start, stop, on_scalar=True):
             left_values = sbuf_tile("left_%s%d" % (block, start), [P, stop - start], F32)
@@ -230,7 +231,6 @@ def tile_picked_phpair_abs_p_kernel(
         left_a = gather_left("A", 0, V)
         empty("B", 0, nc.vector.tensor_copy)
         empty("B", 1, nc.scalar.copy)
-        products("D", 2)
         diff_a = sbuf_tile("diff_a", [P, V], F32, "wB1_codes")
         right_minus_left(diff_a[:], "A", 0, V, left_a[:])
         for half in range(2):
@@ -240,19 +240,21 @@ def tile_picked_phpair_abs_p_kernel(
         for half, (start, stop) in enumerate(PAIR_HALVES):
             right_minus_left(diff_b[:, start:stop], "B", start, stop, gather_left("B", start, stop)[:])
             move(slice(HALF, P), diff_b, half)
-        h["C"] = sbuf_tile("hC", [P, S], F32, "left_A0")
-        for index in range(2):
-            empty("C", index, nc.scalar.copy)
+        empty("C", 0, nc.scalar.copy)
 
         h["D"] = sbuf_tile("hD", [P, S], F32, "left_B0")
         empty("D", 0, nc.scalar.copy)
+        empty("C", 1, nc.scalar.copy)
         empty("D", 1, nc.vector.tensor_copy)
 
         left_of = {}
-        left_of["C", 0] = gather_left("C", 0, V // 2)
-        left_of["D", 0] = gather_left("D", 0, V // 2)
-        left_of["C", 1] = gather_left("C", V // 2, V)
-        left_of["D", 1] = gather_left("D", V // 2, V, on_scalar=False)
+        for block, on_scalar in (("C", True), ("D", False)):
+            left_values = gather_left(block, 0, V // 2, on_scalar)
+            for chunk in range(2):
+                left_of[block, chunk] = left_values[:, chunk * CHUNK : (chunk + 1) * CHUNK]
+        for chunk in range(2, V // CHUNK):
+            for block in "CD":
+                left_of[block, chunk] = gather_left(block, chunk * CHUNK, (chunk + 1) * CHUNK)[:]
 
         z_rounded = [sbuf_tile("z_rounded%d" % a, [P, b - a, PACK], BF16) for a, b in PRODUCTS]
 
@@ -270,9 +272,8 @@ def tile_picked_phpair_abs_p_kernel(
         for chunk in range(V // CHUNK):
             half, inner = divmod(chunk, 2)
             for block in "CD":
-                left_values = left_of[block, half][:, inner * CHUNK : (inner + 1) * CHUNK]
                 dst = diff[half][:, inner, plane[block], :]
-                right_minus_left(dst, block, chunk * CHUNK, (chunk + 1) * CHUNK, left_values)
+                right_minus_left(dst, block, chunk * CHUNK, (chunk + 1) * CHUNK, left_of[block, chunk])
             take_abs(chunk)
 
         def second_product(part, bank, copy):
@@ -292,6 +293,6 @@ def tile_picked_phpair_abs_p_kernel(
             copy(result[:], acc[:])
             nc.sync.dma_start(out[:, start:stop], result[:])
 
-        second_product(0, 4, nc.scalar.copy)
-        second_product(1, 5, nc.scalar.copy)
-        second_product(2, 6, nc.vector.tensor_copy)
+        second_product(0, 0, nc.scalar.copy)
+        second_product(1, 1, nc.scalar.copy)
+        second_product(2, 2, nc.vector.tensor_copy)

@@ -23,10 +23,10 @@ PACK = 4
 PASSES = K // (P * PACK)
 STRIPE = 16
 BANK = 512
-ZEROED_BY_VECTOR = 1216
 PAIR_HALVES = ((0, V // 2), (V // 2, V))
 PRODUCTS = ((0, 256), (256, 384), (384, 512))
 CHUNK = 128
+BY_VECTOR = 1
 CUT = 768
 
 
@@ -66,12 +66,11 @@ def tile_picked_phpair_abs_p_kernel(
             w1_raw[g, half] = dst
             nc.sync.dma_start(dst, w1_parts[g, half])
 
-        nc.vector.memset(scale_table[:, 0:ZEROED_BY_VECTOR].bitcast(I32), 0)
-        nc.gpsimd.memset(scale_table[:, ZEROED_BY_VECTOR:T].bitcast(I32), 0)
+        nc.vector.memset(scale_table[:].bitcast(I32), 0)
         nc.vector.memset(x_scales_mx[:].rearrange("p g s -> p (g s)").bitcast(I32), 0)
 
-        nc.sync.dma_start(offs_sb[:], offs)
         load_words(0, 0, T // 4)
+        nc.sync.dma_start(offs_sb[:], offs)
         nc.sync.dma_start(scale_table[0:P:4, :].bitcast(I32), x_scales.rearrange("z r c -> r z c").bitcast(I32))
         load_words(0, T // 4, T)
         load_words(1, 0, T)
@@ -172,18 +171,21 @@ def tile_picked_phpair_abs_p_kernel(
 
         accs = {}
 
-        def products(block, first_bank):
-            accs[block] = [psum_bank(first_bank + index, BANK) for index in range(2)]
-            for index in range(2):
-                product_pass(accs[block][index], block, 0, index * BANK, (index + 1) * BANK, False)
+        def products(block, banks):
+            accs[block] = [psum_bank(bank, BANK) for bank in banks]
+            product_pass(accs[block][0], block, 0, 0, BANK, False)
+            if block in "AB":
+                product_pass(accs[block][1], block, 0, BANK, S, False)
             product_pass(accs[block][0], block, 1, 0, BANK, True)
+            if block in "CD":
+                product_pass(accs[block][1], block, 0, BANK, S, False)
             product_pass(accs[block][1][:, 0 : CUT - BANK], block, 1, BANK, CUT, False)
             product_pass(accs[block][1][:, CUT - BANK : BANK], block, 1, CUT, S, True)
 
         def empty(block, index, copy):
             copy(h[block][:, index * BANK : (index + 1) * BANK], accs[block][index][:])
 
-        products("A", 0)
+        products("A", (0, 1))
         for index in range(2):
             empty("A", index, nc.scalar.copy)
 
@@ -199,12 +201,14 @@ def tile_picked_phpair_abs_p_kernel(
         round_cd(0, 1, nc.vector.tensor_copy)
         quantize_half("B", 0)
         round_half("B", 1, 1, nc.vector.tensor_copy)
-        round_cd(1, 1, nc.vector.tensor_copy)
+        late = w1_raw[1, 1].rearrange("p j (m t) -> p m j t", t=PACK)[:, :, :, 2:PACK]
+        late_rounded = rounded_cd[1][:, :, 1, :, :].rearrange("p t m j -> p m j t")
+        nc.vector.tensor_copy(late_rounded[:, 0 : HALF // 2], late[:, 0 : HALF // 2])
+        nc.scalar.copy(late_rounded[:, HALF // 2 : HALF], late[:, HALF // 2 : HALF])
         quantize_half("B", 1)
         quantize_cd(0, "rounded_B1")
         quantize_cd(1)
-        for n, block in enumerate("BCD"):
-            products(block, 2 * n + 2)
+        products("B", (2, 3))
 
         def gather_left(block, start, stop, on_scalar=True):
             left_values = sbuf_tile("left_%s%d" % (block, start), [P, stop - start], F32)
@@ -229,32 +233,32 @@ def tile_picked_phpair_abs_p_kernel(
                 )
 
         left_a = gather_left("A", 0, V)
-        empty("B", 0, nc.vector.tensor_copy)
-        empty("B", 1, nc.scalar.copy)
+        for index in range(2):
+            empty("B", index, nc.vector.tensor_copy)
+        products("C", (4, 3))
+        products("D", (6, 7))
         diff_a = sbuf_tile("diff_a", [P, V], F32, "wB1_codes")
         right_minus_left(diff_a[:], "A", 0, V, left_a[:])
         for half in range(2):
             move(slice(0, HALF), diff_a, half)
 
+        empty("C", 0, nc.scalar.copy)
         diff_b = sbuf_tile("diff_b", [P, V], F32)
         for half, (start, stop) in enumerate(PAIR_HALVES):
             right_minus_left(diff_b[:, start:stop], "B", start, stop, gather_left("B", start, stop)[:])
             move(slice(HALF, P), diff_b, half)
-        empty("C", 0, nc.scalar.copy)
 
         h["D"] = sbuf_tile("hD", [P, S], F32, "left_B0")
         empty("D", 0, nc.scalar.copy)
         empty("C", 1, nc.scalar.copy)
         empty("D", 1, nc.vector.tensor_copy)
 
-        left_of = {}
-        for block, on_scalar in (("C", True), ("D", False)):
-            left_values = gather_left(block, 0, V // 2, on_scalar)
-            for chunk in range(2):
-                left_of[block, chunk] = left_values[:, chunk * CHUNK : (chunk + 1) * CHUNK]
-        for chunk in range(2, V // CHUNK):
+        left_d = gather_left("D", 0, BY_VECTOR * CHUNK, on_scalar=False)
+        left_of = {("D", chunk): left_d[:, chunk * CHUNK : (chunk + 1) * CHUNK] for chunk in range(BY_VECTOR)}
+        for chunk in range(V // CHUNK):
             for block in "CD":
-                left_of[block, chunk] = gather_left(block, chunk * CHUNK, (chunk + 1) * CHUNK)[:]
+                if (block, chunk) not in left_of:
+                    left_of[block, chunk] = gather_left(block, chunk * CHUNK, (chunk + 1) * CHUNK)[:]
 
         z_rounded = [sbuf_tile("z_rounded%d" % a, [P, b - a, PACK], BF16) for a, b in PRODUCTS]
 

@@ -26,7 +26,7 @@ BANK = 512
 PAIR_HALVES = ((0, V // 2), (V // 2, V))
 PRODUCTS = ((0, 256), (256, 384), (384, 512))
 CHUNK = 128
-BY_VECTOR = 1
+BY_VECTOR = 2
 CUT = 768
 
 
@@ -89,6 +89,14 @@ def tile_picked_phpair_abs_p_kernel(
             load_weights(w1_rest[:, slot, :, :], g, half)
         nc.sync.dma_start(left_sb[:], left)
         nc.sync.dma_start(right_sb[:], right)
+        w2_codes = sbuf_tile("w2_codes", [P, 2 * N], U8)
+        nc.sync.dma_start(w2_codes[:].bitcast(I32), w2_words[0].bitcast(I32))
+        w2_scales_mx = sbuf_tile("w2_scales_mx", [P, N], U8)
+        nc.vector.memset(w2_scales_mx[:].bitcast(I32), 0)
+        for q in range(4):
+            nc.sync.dma_start(
+                w2_scales_mx[32 * q : 32 * q + 4, :].bitcast(I32), w2_scales[0, 4 * q : 4 * q + 4, :].bitcast(I32)
+            )
 
         picked = {}
 
@@ -163,9 +171,9 @@ def tile_picked_phpair_abs_p_kernel(
         round_half("A", 0, 0, nc.scalar.copy)
         quantize_half("A", 0)
         round_cd(0, 0, nc.scalar.copy)
+        gather_words(1, CUT, S, "rounded_A0")
         round_half("A", 1, 0, nc.scalar.copy)
         quantize_half("A", 1)
-        gather_words(1, CUT, S, "rounded_A1")
         round_cd(1, 0, nc.scalar.copy)
         round_half("B", 0, 1, nc.scalar.copy)
 
@@ -173,11 +181,18 @@ def tile_picked_phpair_abs_p_kernel(
 
         def products(block, banks):
             accs[block] = [psum_bank(bank, BANK) for bank in banks]
+            if block == "D":
+                product_pass(accs[block][1], block, 0, BANK, S, False)
+                product_pass(accs[block][1][:, 0 : CUT - BANK], block, 1, BANK, CUT, False)
+                product_pass(accs[block][1][:, CUT - BANK : BANK], block, 1, CUT, S, True)
+                for g in range(PASSES):
+                    product_pass(accs[block][0], block, g, 0, BANK, g == PASSES - 1)
+                return
             product_pass(accs[block][0], block, 0, 0, BANK, False)
             if block in "AB":
                 product_pass(accs[block][1], block, 0, BANK, S, False)
             product_pass(accs[block][0], block, 1, 0, BANK, True)
-            if block in "CD":
+            if block == "C":
                 product_pass(accs[block][1], block, 0, BANK, S, False)
             product_pass(accs[block][1][:, 0 : CUT - BANK], block, 1, BANK, CUT, False)
             product_pass(accs[block][1][:, CUT - BANK : BANK], block, 1, CUT, S, True)
@@ -188,15 +203,6 @@ def tile_picked_phpair_abs_p_kernel(
         products("A", (0, 1))
         for index in range(2):
             empty("A", index, nc.scalar.copy)
-
-        w2_codes = sbuf_tile("w2_codes", [P, 2 * N], U8, tag="word_table0")
-        nc.sync.dma_start(w2_codes[:].bitcast(I32), w2_words[0].bitcast(I32))
-        w2_scales_mx = sbuf_tile("w2_scales_mx", [P, N], U8, tag="word_table1")
-        nc.gpsimd.memset(w2_scales_mx[:].bitcast(I32), 0)
-        for q in range(4):
-            nc.sync.dma_start(
-                w2_scales_mx[32 * q : 32 * q + 4, :].bitcast(I32), w2_scales[0, 4 * q : 4 * q + 4, :].bitcast(I32)
-            )
 
         round_cd(0, 1, nc.vector.tensor_copy)
         quantize_half("B", 0)
@@ -236,22 +242,22 @@ def tile_picked_phpair_abs_p_kernel(
         for index in range(2):
             empty("B", index, nc.vector.tensor_copy)
         products("C", (4, 3))
-        products("D", (6, 7))
         diff_a = sbuf_tile("diff_a", [P, V], F32, "wB1_codes")
         right_minus_left(diff_a[:], "A", 0, V, left_a[:])
         for half in range(2):
             move(slice(0, HALF), diff_a, half)
 
         empty("C", 0, nc.scalar.copy)
+        products("D", (4, 7))
+        h["D"] = sbuf_tile("hD", [P, S], F32, "left_A0")
         diff_b = sbuf_tile("diff_b", [P, V], F32)
         for half, (start, stop) in enumerate(PAIR_HALVES):
             right_minus_left(diff_b[:, start:stop], "B", start, stop, gather_left("B", start, stop)[:])
             move(slice(HALF, P), diff_b, half)
-
-        h["D"] = sbuf_tile("hD", [P, S], F32, "left_B0")
-        empty("D", 0, nc.scalar.copy)
+            if half == 0:
+                empty("D", 1, nc.vector.tensor_copy)
         empty("C", 1, nc.scalar.copy)
-        empty("D", 1, nc.vector.tensor_copy)
+        empty("D", 0, nc.scalar.copy)
 
         left_d = gather_left("D", 0, BY_VECTOR * CHUNK, on_scalar=False)
         left_of = {("D", chunk): left_d[:, chunk * CHUNK : (chunk + 1) * CHUNK] for chunk in range(BY_VECTOR)}

@@ -27,7 +27,6 @@ PAIR_HALVES = ((0, V // 2), (V // 2, V))
 PRODUCTS = ((0, 256), (256, 384), (384, 512))
 CHUNK = 128
 BY_VECTOR = 2
-CUT = 768
 
 
 def tile_picked_phpair_abs_p_kernel(
@@ -52,7 +51,7 @@ def tile_picked_phpair_abs_p_kernel(
         right_sb = keep.tile([P, V // STRIPE], U16, name="right_sb")
         scale_table = sbuf_tile("scale_table", [P, T], U8)
         scales_picked = sbuf_tile("scales_picked", [P, S], U8)
-        x_scales_mx = sbuf_tile("x_scales_mx", [P, PASSES, S], U8)
+        x_scales_mx = sbuf_tile("x_scales_mx", [P, S], U8)
         word_table = [sbuf_tile("word_table%d" % g, [P, T], I32) for g in range(PASSES)]
 
         w1_parts = w1.rearrange("(g p j) (h c) -> g h p j c", g=PASSES, j=PACK, h=2)
@@ -67,22 +66,25 @@ def tile_picked_phpair_abs_p_kernel(
             nc.sync.dma_start(dst, w1_parts[g, half])
 
         nc.vector.memset(scale_table[:].bitcast(I32), 0)
-        nc.vector.memset(x_scales_mx[:].rearrange("p g s -> p (g s)").bitcast(I32), 0)
 
         load_words(0, 0, T // 4)
         nc.sync.dma_start(offs_sb[:], offs)
-        nc.sync.dma_start(scale_table[0:P:4, :].bitcast(I32), x_scales.rearrange("z r c -> r z c").bitcast(I32))
+        scale_rows = x_scales.rearrange("z (r e) c -> e r z c", e=2)
+        for e in range(2):
+            nc.sync.dma_start(scale_table[e:P:8, :].bitcast(I32), scale_rows[e].bitcast(I32))
         load_words(0, T // 4, T)
         load_words(1, 0, T)
         w1_first = sbuf_tile("w1_first", [P, PACK, H // 2], F32)
         load_weights(w1_first[:], 0, 0)
 
         nc.vector.tensor_copy(scales_picked[:], scale_table[:].indirect(offs_sb[:]))
-        for q in range(4):
-            nc.sync.dma_start(
-                x_scales_mx[32 * q : 32 * q + 4, :, :].rearrange("p g s -> p (g s)").bitcast(I32),
-                scales_picked[32 * q : 32 * q + 32 : 4, :].bitcast(I32),
-            )
+        nc.vector.tensor_copy(x_scales_mx[:].bitcast(I32), scales_picked[:].bitcast(I32))
+        for g in range(PASSES):
+            for e in range(2):
+                nc.sync.dma_start(
+                    x_scales_mx[8 * g + 2 + e : P : 32, :].bitcast(I32),
+                    scales_picked[8 * g + 16 + e : P : 32, :].bitcast(I32),
+                )
 
         w1_rest = sbuf_tile("w1_rest", [P, 3, PACK, H // 2], F32, "scale_table")
         for slot, (g, half) in enumerate(((1, 0), (0, 1), (1, 1))):
@@ -141,37 +143,26 @@ def tile_picked_phpair_abs_p_kernel(
             weights["C", g] = (codes[:, 0:P], scales[:, 0:P])
             weights["D", g] = (codes[:, P : 2 * P], scales[:, P : 2 * P])
 
-        def product_pass(acc, block, g, start, stop, last):
+        def product_pass(acc, block, g, start, stop):
             codes, scales = weights[block, g]
             nc.tensor.matmul_mx(
                 out=acc[:],
                 lhsT=codes.bitcast(FP8X4),
                 lhsT_scale=scales,
                 rhs=picked_words(g, start, stop).bitcast(FP8X4),
-                rhs_scale=x_scales_mx[:, g, start:stop],
+                rhs_scale=x_scales_mx[8 * g : P, start:stop],
                 start=(g == 0),
-                stop=last,
+                stop=(g == PASSES - 1),
             )
 
         h = {block: sbuf_tile("h" + block, [P, S], F32) for block in "ABC"}
 
         gather_words(0, 0, S)
-        unread = psum_bank(7, BANK)
-        for start in (0, BANK):
-            nc.tensor.matmul_mx(
-                out=unread[:],
-                lhsT=picked_words(0, 0, P).bitcast(FP8X4),
-                lhsT_scale=x_scales_mx[:, 0, 0:P],
-                rhs=picked_words(0, start, start + BANK).bitcast(FP8X4),
-                rhs_scale=x_scales_mx[:, 0, start : start + BANK],
-                start=True,
-                stop=True,
-            )
-        gather_words(1, 0, CUT)
+        gather_words(1, 0, BANK)
         round_half("A", 0, 0, nc.scalar.copy)
         quantize_half("A", 0)
         round_cd(0, 0, nc.scalar.copy)
-        gather_words(1, CUT, S, "rounded_A0")
+        gather_words(1, BANK, S, "rounded_A0")
         round_half("A", 1, 0, nc.scalar.copy)
         quantize_half("A", 1)
         round_cd(1, 0, nc.scalar.copy)
@@ -179,28 +170,18 @@ def tile_picked_phpair_abs_p_kernel(
 
         accs = {}
 
-        def products(block, banks):
+        def products(block, banks, steps):
             accs[block] = [psum_bank(bank, BANK) for bank in banks]
-            if block == "D":
-                product_pass(accs[block][1], block, 0, BANK, S, False)
-                product_pass(accs[block][1][:, 0 : CUT - BANK], block, 1, BANK, CUT, False)
-                product_pass(accs[block][1][:, CUT - BANK : BANK], block, 1, CUT, S, True)
-                for g in range(PASSES):
-                    product_pass(accs[block][0], block, g, 0, BANK, g == PASSES - 1)
-                return
-            product_pass(accs[block][0], block, 0, 0, BANK, False)
-            if block in "AB":
-                product_pass(accs[block][1], block, 0, BANK, S, False)
-            product_pass(accs[block][0], block, 1, 0, BANK, True)
-            if block == "C":
-                product_pass(accs[block][1], block, 0, BANK, S, False)
-            product_pass(accs[block][1][:, 0 : CUT - BANK], block, 1, BANK, CUT, False)
-            product_pass(accs[block][1][:, CUT - BANK : BANK], block, 1, CUT, S, True)
+            for index, g in steps:
+                product_pass(accs[block][index], block, g, index * BANK, (index + 1) * BANK)
+
+        pass_by_pass = [(index, g) for g in range(PASSES) for index in range(2)]
+        bank_by_bank = [(index, g) for index in range(2) for g in range(PASSES)]
 
         def empty(block, index, copy):
             copy(h[block][:, index * BANK : (index + 1) * BANK], accs[block][index][:])
 
-        products("A", (0, 1))
+        products("A", (0, 1), pass_by_pass)
         for index in range(2):
             empty("A", index, nc.scalar.copy)
 
@@ -214,7 +195,7 @@ def tile_picked_phpair_abs_p_kernel(
         quantize_half("B", 1)
         quantize_cd(0, "rounded_B1")
         quantize_cd(1)
-        products("B", (2, 3))
+        products("B", (2, 3), pass_by_pass)
 
         def gather_left(block, start, stop, on_scalar=True):
             left_values = sbuf_tile("left_%s%d" % (block, start), [P, stop - start], F32)
@@ -241,14 +222,14 @@ def tile_picked_phpair_abs_p_kernel(
         left_a = gather_left("A", 0, V)
         for index in range(2):
             empty("B", index, nc.vector.tensor_copy)
-        products("C", (4, 3))
+        products("C", (4, 3), bank_by_bank)
         diff_a = sbuf_tile("diff_a", [P, V], F32, "wB1_codes")
         right_minus_left(diff_a[:], "A", 0, V, left_a[:])
         for half in range(2):
             move(slice(0, HALF), diff_a, half)
 
         empty("C", 0, nc.scalar.copy)
-        products("D", (4, 7))
+        products("D", (4, 7), bank_by_bank[2:] + bank_by_bank[:2])
         h["D"] = sbuf_tile("hD", [P, S], F32, "left_A0")
         diff_b = sbuf_tile("diff_b", [P, V], F32)
         for half, (start, stop) in enumerate(PAIR_HALVES):

@@ -158,6 +158,17 @@ def tile_picked_phpair_abs_p_kernel(
         h = {block: sbuf_tile("h" + block, [P, S], F32) for block in "ABC"}
 
         gather_words(0, 0, S)
+        unread = psum_bank(7, BANK)
+        for start in (0, BANK):
+            nc.tensor.matmul_mx(
+                out=unread[:],
+                lhsT=picked_words(0, 0, P).bitcast(FP8X4),
+                lhsT_scale=scales_picked[:, 0:P],
+                rhs=picked_words(0, start, start + BANK).bitcast(FP8X4),
+                rhs_scale=scales_picked[:, start : start + BANK],
+                start=True,
+                stop=True,
+            )
         gather_words(1, 0, BANK)
         round_half("A", 0, 0, nc.scalar.copy)
         quantize_half("A", 0)

@@ -173,7 +173,7 @@ def tile_picked_phpair_abs_p_kernel(
         round_half("A", 0, 0, nc.scalar.copy)
         quantize_half("A", 0)
         round_cd(0, 0, nc.scalar.copy)
-        gather_words(1, BANK, S, "rounded_A0")
+        gather_words(1, BANK, S, "w1_first")
         round_half("A", 1, 0, nc.scalar.copy)
         quantize_half("A", 1)
         round_cd(1, 0, nc.scalar.copy)
@@ -199,12 +199,9 @@ def tile_picked_phpair_abs_p_kernel(
         round_cd(0, 1, nc.vector.tensor_copy)
         quantize_half("B", 0)
         round_half("B", 1, 1, nc.vector.tensor_copy)
-        late = w1_raw[1, 1].rearrange("p j (m t) -> p m j t", t=PACK)[:, :, :, 2:PACK]
-        late_rounded = rounded_cd[1][:, :, 1, :, :].rearrange("p t m j -> p m j t")
-        nc.vector.tensor_copy(late_rounded[:, 0 : HALF // 2], late[:, 0 : HALF // 2])
-        nc.scalar.copy(late_rounded[:, HALF // 2 : HALF], late[:, HALF // 2 : HALF])
+        round_cd(1, 1, nc.vector.tensor_copy)
         quantize_half("B", 1)
-        quantize_cd(0, "rounded_B1")
+        quantize_cd(0, "scale_table")
         quantize_cd(1)
         products("B", (2, 3), pass_by_pass)
 

@@ -61,9 +61,9 @@ def tile_picked_phpair_abs_p_kernel(
             words = x_words[g].rearrange("p n t -> p (n t)").bitcast(I32)
             nc.sync.dma_start(word_table[g][:, start:stop], words[:, start:stop])
 
-        def load_weights(dst, g, half):
-            w1_raw[g, half] = dst
-            nc.sync.dma_start(dst, w1_parts[g, half])
+        def load_part(g, half):
+            w1_raw[g, half] = sbuf_tile("w1_part%d%d" % (g, half), [P, PACK, H // 2], F32)[:]
+            nc.sync.dma_start(w1_raw[g, half], w1_parts[g, half])
 
         nc.vector.memset(scale_table[:].bitcast(I32), 0)
 
@@ -73,9 +73,9 @@ def tile_picked_phpair_abs_p_kernel(
         for e in range(2):
             nc.sync.dma_start(scale_table[e:P:8, :].bitcast(I32), scale_rows[e].bitcast(I32))
         load_words(0, T // 4, T)
+        load_part(0, 0)
         load_words(1, 0, T)
-        w1_first = sbuf_tile("w1_first", [P, PACK, H // 2], F32)
-        load_weights(w1_first[:], 0, 0)
+        load_part(1, 0)
 
         nc.vector.tensor_copy(scales_picked[:], scale_table[:].indirect(offs_sb[:]))
         nc.vector.tensor_copy(x_scales_mx[:].bitcast(I32), scales_picked[:].bitcast(I32))
@@ -86,9 +86,8 @@ def tile_picked_phpair_abs_p_kernel(
                     scales_picked[8 * g + 16 + e : P : 32, :].bitcast(I32),
                 )
 
-        w1_rest = sbuf_tile("w1_rest", [P, 3, PACK, H // 2], F32, "scale_table")
-        for slot, (g, half) in enumerate(((1, 0), (0, 1), (1, 1))):
-            load_weights(w1_rest[:, slot, :, :], g, half)
+        for g in range(PASSES):
+            load_part(g, 1)
         nc.sync.dma_start(left_sb[:], left)
         nc.sync.dma_start(right_sb[:], right)
         w2_codes = sbuf_tile("w2_codes", [P, 2 * N], U8)
@@ -155,25 +154,24 @@ def tile_picked_phpair_abs_p_kernel(
                 stop=(g == PASSES - 1),
             )
 
-        h = {block: sbuf_tile("h" + block, [P, S], F32) for block in "ABC"}
+        h = {block: sbuf_tile("h" + block, [P, S], F32) for block in "BC"}
 
         gather_words(0, 0, S)
         unread = psum_bank(7, BANK)
-        for start in (0, BANK):
+        for start, stop in ((0, BANK), (BANK, BANK + BANK // 2)):
             nc.tensor.matmul_mx(
-                out=unread[:],
+                out=unread[:, 0 : stop - start],
                 lhsT=picked_words(0, 0, P).bitcast(FP8X4),
                 lhsT_scale=scales_picked[:, 0:P],
-                rhs=picked_words(0, start, start + BANK).bitcast(FP8X4),
-                rhs_scale=scales_picked[:, start : start + BANK],
+                rhs=picked_words(0, start, stop).bitcast(FP8X4),
+                rhs_scale=scales_picked[:, start:stop],
                 start=True,
                 stop=True,
             )
-        gather_words(1, 0, BANK)
         round_half("A", 0, 0, nc.scalar.copy)
         quantize_half("A", 0)
         round_cd(0, 0, nc.scalar.copy)
-        gather_words(1, BANK, S, "w1_first")
+        gather_words(1, 0, S)
         round_half("A", 1, 0, nc.scalar.copy)
         quantize_half("A", 1)
         round_cd(1, 0, nc.scalar.copy)
@@ -193,6 +191,7 @@ def tile_picked_phpair_abs_p_kernel(
             copy(h[block][:, index * BANK : (index + 1) * BANK], accs[block][index][:])
 
         products("A", (0, 1), pass_by_pass)
+        h["A"] = sbuf_tile("hA", [P, S], F32, "w1_part01")
         for index in range(2):
             empty("A", index, nc.scalar.copy)
 
@@ -201,7 +200,7 @@ def tile_picked_phpair_abs_p_kernel(
         round_half("B", 1, 1, nc.vector.tensor_copy)
         round_cd(1, 1, nc.vector.tensor_copy)
         quantize_half("B", 1)
-        quantize_cd(0, "scale_table")
+        quantize_cd(0, "w1_part11")
         quantize_cd(1)
         products("B", (2, 3), pass_by_pass)
 

@@ -157,17 +157,6 @@ def tile_picked_phpair_abs_p_kernel(
         h = {block: sbuf_tile("h" + block, [P, S], F32) for block in "BC"}
 
         gather_words(0, 0, S)
-        unread = psum_bank(7, BANK)
-        for start, stop in ((0, BANK), (BANK, BANK + BANK // 2)):
-            nc.tensor.matmul_mx(
-                out=unread[:, 0 : stop - start],
-                lhsT=picked_words(0, 0, P).bitcast(FP8X4),
-                lhsT_scale=scales_picked[:, 0:P],
-                rhs=picked_words(0, start, stop).bitcast(FP8X4),
-                rhs_scale=scales_picked[:, start:stop],
-                start=True,
-                stop=True,
-            )
         round_half("A", 0, 0, nc.scalar.copy)
         quantize_half("A", 0)
         round_cd(0, 0, nc.scalar.copy)

@@ -23,7 +23,7 @@ PACK = 4
 PASSES = K // (P * PACK)
 STRIPE = 16
 BANK = 512
-PAIR_HALVES = ((0, V // 2), (V // 2, V))
+B_PIECES = ((0, 128), (128, 384), (384, V))
 PRODUCTS = ((0, 256), (256, 384), (384, 512))
 CHUNK = 128
 BY_VECTOR = 2
@@ -205,14 +205,13 @@ def tile_picked_phpair_abs_p_kernel(
         def right_minus_left(dst, block, start, stop, left_values):
             nc.vector.tensor_tensor(dst, h[block][:].indirect(entries(right_sb, start, stop)), left_values, SUB)
 
-        diff = [sbuf_tile("diff%d" % half, [P, 2, PACK, CHUNK], F32) for half in range(2)]
+        diff = sbuf_tile("diff", [P, V // CHUNK, PACK, CHUNK], F32)
 
-        def move(partitions, block_diff, half):
-            start, stop = PAIR_HALVES[half]
+        def move(partitions, block_diff, start, stop):
             for t in range(2):
                 nc.sync.dma_start(
-                    diff[half][partitions, :, t, :],
-                    block_diff[HALF * t : HALF * (t + 1), start:stop].rearrange("p (c v) -> p c v", c=2),
+                    diff[partitions, start // CHUNK : stop // CHUNK, t, :],
+                    block_diff[HALF * t : HALF * (t + 1), start:stop].rearrange("p (c v) -> p c v", v=CHUNK),
                 )
 
         left_a = gather_left("A", 0, V)
@@ -221,17 +220,16 @@ def tile_picked_phpair_abs_p_kernel(
         products("C", (4, 3), bank_by_bank)
         diff_a = sbuf_tile("diff_a", [P, V], F32, "wB1_codes")
         right_minus_left(diff_a[:], "A", 0, V, left_a[:])
-        for half in range(2):
-            move(slice(0, HALF), diff_a, half)
+        move(slice(0, HALF), diff_a, 0, V)
 
         empty("C", 0, nc.scalar.copy)
         products("D", (4, 7), bank_by_bank[2:] + bank_by_bank[:2])
         h["D"] = sbuf_tile("hD", [P, S], F32, "left_A0")
         diff_b = sbuf_tile("diff_b", [P, V], F32)
-        for half, (start, stop) in enumerate(PAIR_HALVES):
+        for half, (start, stop) in enumerate(B_PIECES):
             right_minus_left(diff_b[:, start:stop], "B", start, stop, gather_left("B", start, stop)[:])
-            move(slice(HALF, P), diff_b, half)
-            if half == 0:
+            move(slice(HALF, P), diff_b, start, stop)
+            if half == 1:
                 empty("D", 1, nc.vector.tensor_copy)
         empty("C", 1, nc.scalar.copy)
         empty("D", 0, nc.scalar.copy)
@@ -251,19 +249,18 @@ def tile_picked_phpair_abs_p_kernel(
             offset = first - PRODUCTS[part][0]
             nc.scalar.activation(
                 z_rounded[part][:, offset : offset + CHUNK, :].rearrange("p (c i) t -> p c t i", i=4),
-                diff[chunk // 2][:, chunk % 2, :, :].rearrange("p t (c i) -> p c t i", i=4),
+                diff[:, chunk, :, :].rearrange("p t (c i) -> p c t i", i=4),
                 ABS,
             )
 
         plane = {"C": 2, "D": 3}
         for chunk in range(V // CHUNK):
-            half, inner = divmod(chunk, 2)
             for block in "CD":
-                dst = diff[half][:, inner, plane[block], :]
+                dst = diff[:, chunk, plane[block], :]
                 right_minus_left(dst, block, chunk * CHUNK, (chunk + 1) * CHUNK, left_of[block, chunk])
             take_abs(chunk)
 
-        def second_product(part, bank, copy):
+        def second_product(part, bank, copy, tag=None):
             start, stop = PRODUCTS[part]
             codes, scales = quantize("z%d" % part, z_rounded[part][:].rearrange("p v t -> p (v t)"), stop - start)
             acc = psum_bank(bank, stop - start)
@@ -276,10 +273,10 @@ def tile_picked_phpair_abs_p_kernel(
                 start=True,
                 stop=True,
             )
-            result = sbuf_tile("result%d" % part, [P, stop - start], F32)
+            result = sbuf_tile("result%d" % part, [P, stop - start], F32, tag)
             copy(result[:], acc[:])
             nc.sync.dma_start(out[:, start:stop], result[:])
 
-        second_product(0, 0, nc.scalar.copy)
+        second_product(0, 0, nc.scalar.copy, "diff")
         second_product(1, 1, nc.scalar.copy)
         second_product(2, 2, nc.vector.tensor_copy)

from contextlib import ExitStack

import concourse.mybir as mybir

K, T, S, H, N, V = 1024, 2048, 1024, 512, 128, 512
FLOPS = 2 * K * H * S + 2 * H * N * V

F32 = mybir.dt.float32
BF16 = mybir.dt.bfloat16
I32 = mybir.dt.int32
U32 = mybir.dt.uint32
U16 = mybir.dt.uint16
U8 = mybir.dt.uint8
FP8X4 = mybir.dt.float8_e4m3fn_x4
FP4X4 = mybir.dt.float4_e2m1fn_x4
ABS = mybir.ActivationFunctionType.Abs
COPY = mybir.ActivationFunctionType.Copy
SUB = mybir.AluOpType.subtract

P = 128
HALF = P // 2
PACK = 4
PASSES = K // (P * PACK)
STRIPE = 16
BANK = 512
B_PIECES = ((0, 128), (128, 384), (384, V))
PRODUCTS = ((0, 256), (256, 384), (384, 512))
CHUNK = 128
BY_VECTOR = 2


def tile_picked_phpair_abs_p_kernel(
    tc, x_words, x_scales, w1, w2_words, w2_scales, offs, left, right, out
):
    nc = tc.nc
    with ExitStack() as ctx:
        keep = ctx.enter_context(tc.tile_pool(name="keep", bufs=1))
        psum = ctx.enter_context(tc.psum_pool(name="psum", bufs=1))

        def sbuf_tile(name, shape, dtype, tag=None):
            return keep.tile(shape, dtype, name=name, tag=tag or name, align_bytes=64)

        def psum_bank(index, width):
            return psum.tile([P, width], F32, name="bank%d" % index)

        def entries(list_tile, start, stop):
            return list_tile[:, start // STRIPE : stop // STRIPE]

        offs_sb = keep.tile([P, S // STRIPE], U16, name="offs_sb")
        left_sb = keep.tile([P, V // STRIPE], U16, name="left_sb")
        right_sb = keep.tile([P, V // STRIPE], U16, name="right_sb")
        scale_table = sbuf_tile("scale_table", [P, T], U8)
        scales_picked = sbuf_tile("scales_picked", [P, S], U8)
        x_scales_mx = sbuf_tile("x_scales_mx", [P, S], U8)
        word_table = [sbuf_tile("word_table%d" % g, [P, T], I32) for g in range(PASSES)]

        w1_parts = w1.rearrange("(g p j) (h c) -> g h p j c", g=PASSES, j=PACK, h=2)
        w1_raw = {}

        def load_words(g, start, stop):
            words = x_words[g].rearrange("p n t -> p (n t)").bitcast(I32)
            nc.sync.dma_start(word_table[g][:, start:stop], words[:, start:stop])

        def load_part(g, half):
            w1_raw[g, half] = sbuf_tile("w1_part%d%d" % (g, half), [P, PACK, H // 2], F32)[:]
            nc.sync.dma_start(w1_raw[g, half], w1_parts[g, half])

        nc.vector.memset(scale_table[:].bitcast(I32), 0)

        load_words(0, 0, T // 4)
        nc.sync.dma_start(offs_sb[:], offs)
        scale_rows = x_scales.rearrange("z (r e) c -> e r z c", e=2)
        for e in range(2):
            nc.sync.dma_start(scale_table[e:P:8, :].bitcast(I32), scale_rows[e].bitcast(I32))
        load_words(0, T // 4, T)
        load_part(0, 0)
        load_words(1, 0, T)
        load_part(1, 0)

        nc.vector.tensor_copy(scales_picked[:], scale_table[:].indirect(offs_sb[:]))
        nc.vector.tensor_copy(x_scales_mx[:].bitcast(I32), scales_picked[:].bitcast(I32))
        for g in range(PASSES):
            for e in range(2):
                nc.sync.dma_start(
                    x_scales_mx[8 * g + 2 + e : P : 32, :].bitcast(I32),
                    scales_picked[8 * g + 16 + e : P : 32, :].bitcast(I32),
                )

        for g in range(PASSES):
            load_part(g, 1)
        nc.sync.dma_start(left_sb[:], left)
        nc.sync.dma_start(right_sb[:], right)
        w2_codes = sbuf_tile("w2_codes", [P, 2 * N], U8)
        nc.sync.dma_start(w2_codes[:].bitcast(I32), w2_words[0].bitcast(I32))
        w2_scales_mx = sbuf_tile("w2_scales_mx", [P, N], U8)
        nc.vector.memset(w2_scales_mx[:].bitcast(I32), 0)
        for q in range(4):
            nc.sync.dma_start(
                w2_scales_mx[32 * q : 32 * q + 4, :].bitcast(I32), w2_scales[0, 4 * q : 4 * q + 4, :].bitcast(I32)
            )

        picked = {}

        def gather_words(g, start, stop, tag=None):
            words = sbuf_tile("words_picked%d_%d" % (g, start), [P, stop - start], U32, tag)
            nc.vector.tensor_copy(words[:], word_table[g][:].bitcast(U32).indirect(entries(offs_sb, start, stop)))
            picked[g, start] = words

        def picked_words(g, start, stop):
            first = max(key[1] for key in picked if key[0] == g and key[1] <= start)
            return picked[g, first][:, start - first : stop - first]

        def round_weights(dst, g, half, first_plane, copy):
            src = w1_raw[g, half].rearrange("p j (m t) -> p m j t", t=PACK)[:, :, :, first_plane : first_plane + 2]
            copy(dst.rearrange("p t m j -> p m j t"), src)

        def quantize(name, rounded, width, tag=None):
            codes = sbuf_tile(name + "_codes", [P, width], U32, tag)
            scales = sbuf_tile(name + "_scales", [P, width], U8)
            nc.vector.quantize_mx(out=codes[:].bitcast(FP8X4), scales=scales[:], in_=rounded)
            return codes, scales

        weights = {}
        rounded = {}

        def round_half(block, g, half, copy):
            rounded[block, g] = sbuf_tile("rounded_%s%d" % (block, g), [P, 2, HALF, PACK], BF16)
            round_weights(rounded[block, g][:], g, half, 0, copy)

        def quantize_half(block, g):
            codes, scales = quantize("w%s%d" % (block, g), rounded[block, g][:].rearrange("p t m j -> p (t m j)"), P)
            weights[block, g] = (codes[:], scales[:])

        rounded_cd = [sbuf_tile("rounded_cd%d" % g, [P, 2, 2, HALF, PACK], BF16) for g in range(PASSES)]

        def round_cd(g, half, copy):
            round_weights(rounded_cd[g][:, :, half, :, :], g, half, 2, copy)

        def quantize_cd(g, tag=None):
            flat = rounded_cd[g][:].rearrange("p t h m j -> p (t h m j)")
            codes, scales = quantize("wCD%d" % g, flat, 2 * P, tag)
            weights["C", g] = (codes[:, 0:P], scales[:, 0:P])
            weights["D", g] = (codes[:, P : 2 * P], scales[:, P : 2 * P])

        def product_pass(acc, block, g, start, stop):
            codes, scales = weights[block, g]
            nc.tensor.matmul_mx(
                out=acc[:],
                lhsT=codes.bitcast(FP8X4),
                lhsT_scale=scales,
                rhs=picked_words(g, start, stop).bitcast(FP8X4),
                rhs_scale=x_scales_mx[8 * g : P, start:stop],
                start=(g == 0),
                stop=(g == PASSES - 1),
            )

        h = {block: sbuf_tile("h" + block, [P, S], F32) for block in "BC"}

        gather_words(0, 0, S)
        round_half("A", 0, 0, nc.scalar.copy)
        quantize_half("A", 0)
        round_cd(0, 0, nc.scalar.copy)
        gather_words(1, 0, S)
        round_half("A", 1, 0, nc.scalar.copy)
        quantize_half("A", 1)
        round_cd(1, 0, nc.scalar.copy)
        round_half("B", 0, 1, nc.scalar.copy)

        accs = {}

        def products(block, banks, steps):
            accs[block] = [psum_bank(bank, BANK) for bank in banks]
            for index, g in steps:
                product_pass(accs[block][index], block, g, index * BANK, (index + 1) * BANK)

        pass_by_pass = [(index, g) for g in range(PASSES) for index in range(2)]
        bank_by_bank = [(index, g) for index in range(2) for g in range(PASSES)]

        def empty(block, index, copy):
            copy(h[block][:, index * BANK : (index + 1) * BANK], accs[block][index][:])

        products("A", (0, 1), pass_by_pass)
        h["A"] = sbuf_tile("hA", [P, S], F32, "w1_part01")
        for index in range(2):
            empty("A", index, nc.scalar.copy)

        round_cd(0, 1, nc.vector.tensor_copy)
        quantize_half("B", 0)
        round_half("B", 1, 1, nc.vector.tensor_copy)
        round_cd(1, 1, nc.vector.tensor_copy)
        quantize_half("B", 1)
        quantize_cd(0, "w1_part11")
        quantize_cd(1)
        products("B", (2, 3), pass_by_pass)

        def gather_left(block, start, stop, on_scalar=True):
            left_values = sbuf_tile("left_%s%d" % (block, start), [P, stop - start], F32)
            window = h[block][:].indirect(entries(left_sb, start, stop))
            if on_scalar:
                nc.scalar.activation(left_values[:], window, COPY)
            else:
                nc.vector.tensor_copy(left_values[:], window)
            return left_values

        def right_minus_left(dst, block, start, stop, left_values):
            nc.vector.tensor_tensor(dst, h[block][:].indirect(entries(right_sb, start, stop)), left_values, SUB)

        diff = sbuf_tile("diff", [P, V // CHUNK, PACK, CHUNK], F32)

        def move(partitions, block_diff, start, stop):
            for t in range(2):
                nc.sync.dma_start(
                    diff[partitions, start // CHUNK : stop // CHUNK, t, :],
                    block_diff[HALF * t : HALF * (t + 1), start:stop].rearrange("p (c v) -> p c v", v=CHUNK),
                )

        left_a = gather_left("A", 0, V)
        for index in range(2):
            empty("B", index, nc.vector.tensor_copy)
        products("C", (4, 3), bank_by_bank)
        diff_a = sbuf_tile("diff_a", [P, V], F32, "wB1_codes")
        right_minus_left(diff_a[:], "A", 0, V, left_a[:])
        move(slice(0, HALF), diff_a, 0, V)

        empty("C", 0, nc.scalar.copy)
        products("D", (4, 7), bank_by_bank[2:] + bank_by_bank[:2])
        h["D"] = sbuf_tile("hD", [P, S], F32, "left_A0")
        diff_b = sbuf_tile("diff_b", [P, V], F32)
        for half, (start, stop) in enumerate(B_PIECES):
            right_minus_left(diff_b[:, start:stop], "B", start, stop, gather_left("B", start, stop)[:])
            move(slice(HALF, P), diff_b, start, stop)
            if half == 1:
                empty("D", 1, nc.vector.tensor_copy)
        empty("C", 1, nc.scalar.copy)
        empty("D", 0, nc.scalar.copy)

        left_d = gather_left("D", 0, BY_VECTOR * CHUNK, on_scalar=False)
        left_of = {("D", chunk): left_d[:, chunk * CHUNK : (chunk + 1) * CHUNK] for chunk in range(BY_VECTOR)}
        for chunk in range(V // CHUNK):
            for block in "CD":
                if (block, chunk) not in left_of:
                    left_of[block, chunk] = gather_left(block, chunk * CHUNK, (chunk + 1) * CHUNK)[:]

        z_rounded = [sbuf_tile("z_rounded%d" % a, [P, b - a, PACK], BF16) for a, b in PRODUCTS]

        def take_abs(chunk):
            first = chunk * CHUNK
            part = max(index for index, (a, b) in enumerate(PRODUCTS) if a <= first)
            offset = first - PRODUCTS[part][0]
            nc.scalar.activation(
                z_rounded[part][:, offset : offset + CHUNK, :].rearrange("p (c i) t -> p c t i", i=4),
                diff[:, chunk, :, :].rearrange("p t (c i) -> p c t i", i=4),
                ABS,
            )

        plane = {"C": 2, "D": 3}
        for chunk in range(V // CHUNK):
            for block in "CD":
                dst = diff[:, chunk, plane[block], :]
                right_minus_left(dst, block, chunk * CHUNK, (chunk + 1) * CHUNK, left_of[block, chunk])
            take_abs(chunk)

        def second_product(part, bank, copy, tag=None):
            start, stop = PRODUCTS[part]
            codes, scales = quantize("z%d" % part, z_rounded[part][:].rearrange("p v t -> p (v t)"), stop - start)
            acc = psum_bank(bank, stop - start)
            nc.tensor.matmul_mx(
                out=acc[:],
                lhsT=w2_codes[:].bitcast(FP4X4),
                lhsT_scale=w2_scales_mx[:],
                rhs=codes[:].bitcast(FP8X4),
                rhs_scale=scales[:],
                start=True,
                stop=True,
            )
            result = sbuf_tile("result%d" % part, [P, stop - start], F32, tag)
            copy(result[:], acc[:])
            nc.sync.dma_start(out[:, start:stop], result[:])

        second_product(0, 0, nc.scalar.copy, "diff")
        second_product(1, 1, nc.scalar.copy)
        second_product(2, 2, nc.vector.tensor_copy)
